import numpy as np
import ml_dtypes


def mxq(x, axis, fmt="e4m3"):
    dtype, down = {"e4m3": (ml_dtypes.float8_e4m3fn, 7), "e5m2": (ml_dtypes.float8_e5m2, 14)}[fmt]
    v = np.moveaxis(np.asarray(x, np.float32).astype(ml_dtypes.bfloat16).astype(np.float64), axis, -1)
    blocks = v.reshape(v.shape[:-1] + (-1, 32))
    amax = np.abs(blocks).max(-1, keepdims=True)
    byte = np.maximum(np.where(amax > 0, np.frexp(amax)[1] - 1 + 127, 0) - down, 1)
    scale = np.exp2(byte - 127.0)
    codes = (blocks / scale).astype(np.float32).astype(dtype).astype(np.float64)
    return np.moveaxis((codes * scale).reshape(v.shape), -1, axis)


WIDE = False


def mx_kscale(k):
    if not WIDE:
        return np.ones(k)
    levels = np.array([10, -10, 5, -5, 0])
    if k % 512:
        return np.exp2(np.random.permutation(np.resize(levels, k // 32))).repeat(32)
    a = np.empty((k // 512, 16))
    for p in range(k // 512):
        a[p, :8] = np.random.permutation(np.resize(levels, 8))
        for g in range(8):
            far = levels[np.abs(levels - a[p, g]) >= 10]
            a[p, g + 8] = far[np.random.randint(len(far))]
    return np.exp2(a.ravel()).repeat(32)


def f64(x):
    return np.asarray(x).astype(np.float64)


def striped(idx):
    return np.tile(idx.reshape(-1, 16).T, (8, 1)).astype(np.uint16)


def unstriped(offs):
    return offs[:16].T.reshape(-1).astype(np.int64)


E2M1 = np.array([0.0, 0.5, 1.0, 1.5, 2.0, 3.0, 4.0, 6.0, -0.0, -0.5, -1.0, -1.5, -2.0, -3.0, -4.0, -6.0])


def pack_weight(w, fmt):
    k, n = w.shape
    w = f64(np.asarray(w, np.float32).astype(ml_dtypes.bfloat16)).reshape(k // 32, 32, n)
    amax = np.abs(w).max(1)
    if fmt == "e4m3":
        byte = np.frexp(amax)[1] - 1 + 127 - 7
    else:
        mant, ex = np.frexp(amax / 6.0)
        byte = np.where(mant > 0.5, ex, ex - 1) + 127
    byte = np.clip(np.where(amax > 0, byte, 1), 1, 254)
    scaled = (w * np.exp2(127.0 - byte)[:, None, :]).reshape(k, n).astype(np.float32)
    by_word = np.ascontiguousarray(scaled.reshape(k // 512, 128, 4, n).transpose(0, 1, 3, 2))
    if fmt == "e4m3":
        words = by_word.astype(ml_dtypes.float8_e4m3fn).view(np.uint8)
    else:
        c = by_word.astype(ml_dtypes.float4_e2m1fn).view(np.uint8) & 0xF
        words = (c[..., 0::2] | (c[..., 1::2] << 4)).reshape(k // 512, 128, 2 * n)
    return np.ascontiguousarray(words), np.ascontiguousarray(byte.astype(np.uint8).reshape(k // 512, 16, n))


def unpack_weight(words, scales, fmt):
    g, _, n = scales.shape
    words = np.ascontiguousarray(words).reshape(g, 128, n, -1)
    if fmt == "e4m3":
        vals = words.view(ml_dtypes.float8_e4m3fn).astype(np.float64)
    else:
        nib = np.empty((g, 128, n, 4), np.uint8)
        nib[..., 0::2] = words & 0xF
        nib[..., 1::2] = words >> 4
        vals = E2M1[nib]
    vals = vals * np.repeat(np.exp2(scales.astype(np.float64) - 127.0), 8, axis=1)[..., None]
    return vals.transpose(0, 1, 3, 2).reshape(g * 512, n)


def relu(v):
    return np.maximum(v, 0.0)


K, T, S, H, N = 512, 2048, 1024, 512, 256


def setup_inputs():
    n = np.random.standard_normal
    s = mx_kscale(K)
    u = mx_kscale(H)
    hard = np.random.permutation(T)[:S]
    x = pack_weight(n((K, T)) * s[:, None], "e4m3")
    w = pack_weight(n((K, N)) / np.sqrt(K) / s[:, None], "e2m1")
    w1 = pack_weight(n((K, H)) / np.sqrt(K) / s[:, None], "e2m1")
    w3 = pack_weight(n((K, H)) / np.sqrt(K) / s[:, None] * u, "e2m1")
    w2 = pack_weight(n((H, N)) / np.sqrt(H) / u[:, None], "e2m1")
    return {
        "x_words": x[0],
        "x_scales": x[1],
        "w_words": w[0],
        "w_scales": w[1],
        "w1_words": w1[0],
        "w1_scales": w1[1],
        "w3_words": w3[0],
        "w3_scales": w3[1],
        "w2_words": w2[0],
        "w2_scales": w2[1],
        "offs": striped(hard),
    }


def reference(x_words, x_scales, w_words, w_scales, w1_words, w1_scales, w3_words, w3_scales, w2_words, w2_scales, offs):
    w = unpack_weight(w_words, w_scales, "e2m1")
    w1 = unpack_weight(w1_words, w1_scales, "e2m1")
    w3 = unpack_weight(w3_words, w3_scales, "e2m1")
    w2 = unpack_weight(w2_words, w2_scales, "e2m1")
    idx = unstriped(offs)
    x = unpack_weight(x_words, x_scales, "e4m3")
    out = w.T @ x
    h = relu(w1.T @ x[:, idx]) * (w3.T @ x[:, idx])
    out[:, idx] = w2.T @ mxq(h, 0, "e4m3")
    return out

@@ -1,0 +1,177 @@
+from contextlib import ExitStack
+
+import concourse.mybir as mybir
+
+K, T, S, H, N = 512, 2048, 1024, 512, 256
+FLOPS = 2 * K * N * T + 2 * 2 * K * H * S + 2 * H * N * S
+
+F32 = mybir.dt.float32
+BF16 = mybir.dt.bfloat16
+I32 = mybir.dt.int32
+U32 = mybir.dt.uint32
+U16 = mybir.dt.uint16
+U8 = mybir.dt.uint8
+FP8X4 = mybir.dt.float8_e4m3fn_x4
+FP4X4 = mybir.dt.float4_e2m1fn_x4
+ALU = mybir.AluOpType
+
+P = 128
+PACK = 4
+BANK = 512
+BLOCK = 128
+CHUNK = 256
+PER_COL = 16
+
+
+def load_scale_rows(queue, plane, rows):
+    by_quadrant = rows.rearrange("(q r) c -> r q c", r=4)
+    for r in range(4):
+        queue.dma_start(out=plane[r:P:32, :].bitcast(I32), in_=by_quadrant[r].bitcast(I32))
+
+
+def tile_moe_cas_glu_relu_kernel(
+    tc, x_words, x_scales, w_words, w_scales, w1_words, w1_scales, w3_words, w3_scales, w2_words, w2_scales, offs, out
+):
+    nc = tc.nc
+    chunks = S // CHUNK
+    with ExitStack() as ctx:
+        keep = ctx.enter_context(tc.tile_pool(name="keep", bufs=1))
+        ring = ctx.enter_context(tc.tile_pool(name="ring", bufs=3))
+        psum = ctx.enter_context(tc.psum_pool(name="psum", bufs=2))
+
+        offsets = keep.tile([P, S // PER_COL], U16, name="offsets")
+        xw = keep.tile([P, T], I32, name="xw", align_bytes=64)
+        xs = keep.tile([P, T], U8, name="xs", align_bytes=64)
+        up_raw = keep.tile([P, 2, 2 * H], U8, name="up_raw", align_bytes=64)
+        up = keep.tile([P, 2 * 2 * H], U8, name="up", align_bytes=64)
+        ws = keep.tile([P, 2 * H + 2 * N], U8, name="ws", align_bytes=64)
+        ups = keep.tile([P, 2 * H], U8, name="ups", align_bytes=64)
+        ww = keep.tile([P, 2 * N], U8, name="ww", align_bytes=64)
+        w2w = keep.tile([P, 2 * N], U8, name="w2w", align_bytes=64)
+
+        nc.vector.memset(xs[:].bitcast(I32), 0)
+        nc.vector.memset(ws[:].bitcast(I32), 0)
+
+        nc.sync.dma_start(offsets[:], offs)
+        nc.sync.dma_start(out=up_raw[:, 1, :].bitcast(I32), in_=w3_words[0].bitcast(I32))
+        nc.sync.dma_start(out=up_raw[:, 0, :].bitcast(I32), in_=w1_words[0].bitcast(I32))
+        load_scale_rows(nc.scalar, xs, x_scales[0])
+        nc.sync.dma_start(out=xw[:], in_=x_words[0].rearrange("p t d -> p (t d)").bitcast(I32))
+        nc.gpsimd.dma_start(out=ww[:].bitcast(I32), in_=w_words[0].bitcast(I32))
+        nc.gpsimd.dma_start(out=w2w[:].bitcast(I32), in_=w2_words[0].bitcast(I32))
+        load_scale_rows(nc.scalar, ws[:, H : 2 * H], w3_scales[0])
+        load_scale_rows(nc.sync, ws[:, 0:H], w1_scales[0])
+        load_scale_rows(nc.sync, ws[:, 2 * H : 2 * H + N], w_scales[0])
+        load_scale_rows(nc.sync, ws[:, 2 * H + N :], w2_scales[0])
+        w_plane = ws[:, 2 * H : 2 * H + N]
+        w2_plane = ws[:, 2 * H + N :]
+
+        def list_part(first, count):
+            return offsets[:, first // PER_COL : (first + count) // PER_COL]
+
+        gs = [keep.tile([P, 2 * CHUNK], U8, name="gs%d" % c, align_bytes=64) for c in range(chunks // 2)]
+        gw = [keep.tile([P, CHUNK], U32, name="gw%d" % c, align_bytes=64) for c in range(chunks)]
+        for c in range(chunks // 2):
+            nc.vector.tensor_copy(gs[c][:], xs[:].indirect(list_part(2 * c * CHUNK, 2 * CHUNK)))
+
+        nc.vector.tensor_copy(
+            out=up[:].bitcast(U16).rearrange("p (w t m) -> p w t m", w=2, t=PACK),
+            in_=up_raw[:].bitcast(U16).rearrange("p w (m t) -> p w t m", t=PACK),
+        )
+        nc.vector.tensor_copy(gw[0][:], xw[:].bitcast(U32).indirect(list_part(0, CHUNK)))
+        for matrix in (1, 0):
+            cols = slice(matrix * H, (matrix + 1) * H)
+            nc.vector.tensor_copy(
+                out=ups[:, cols].rearrange("p (t m) -> p t m", t=PACK),
+                in_=ws[:, cols].rearrange("p (m t) -> p t m", t=PACK),
+            )
+        for c in range(1, chunks):
+            nc.vector.tensor_copy(gw[c][:], xw[:].bitcast(U32).indirect(list_part(c * CHUNK, CHUNK)))
+
+        window = [keep.tile([P, T], F32, name="window%d" % b) for b in range(N // P)]
+
+        def light(b, j):
+            cols = slice(j * BANK, (j + 1) * BANK)
+            acc = psum.tile([P, BANK], F32, name="light")
+            nc.tensor.matmul_mx(
+                out=acc[:],
+                lhsT=ww[:, 2 * P * b : 2 * P * (b + 1)].bitcast(FP4X4),
+                lhsT_scale=w_plane[:, P * b : P * (b + 1)],
+                rhs=xw[:, cols].bitcast(FP8X4),
+                rhs_scale=xs[:, cols],
+                start=True,
+                stop=True,
+            )
+            nc.scalar.copy(out=window[b][:, cols], in_=acc[:])
+
+        def first_layer(matrix, block):
+            c, lo = divmod(block * BLOCK, CHUNK)
+            c2, lo2 = divmod(block * BLOCK, 2 * CHUNK)
+            acc = psum.tile([P, PACK, BLOCK], F32, name="pre%d" % matrix)
+            for t in range(PACK):
+                col = matrix * H + t * P
+                nc.tensor.matmul_mx(
+                    out=acc[:, t, :],
+                    lhsT=up[:, 2 * col : 2 * (col + P)].bitcast(FP4X4),
+                    lhsT_scale=ups[:, col : col + P],
+                    rhs=gw[c][:, lo : lo + BLOCK].bitcast(FP8X4),
+                    rhs_scale=gs[c2][:, lo2 : lo2 + BLOCK],
+                    start=True,
+                    stop=True,
+                )
+            return acc
+
+        hidden = [keep.tile([P, CHUNK * PACK], BF16, name="hidden%d" % c, align_bytes=64) for c in range(chunks)]
+
+        def gate(block):
+            c, lo = divmod(block * BLOCK, CHUNK)
+            lin = first_layer(1, block)
+            lin_sb = ring.tile([P, BLOCK, PACK], F32, name="lin_sb")
+            nc.scalar.copy(out=lin_sb[:], in_=lin[:].rearrange("p t n -> p n t"))
+            pre = first_layer(0, block)
+            nc.vector.scalar_tensor_tensor(
+                out=hidden[c][:, lo * PACK : (lo + BLOCK) * PACK].rearrange("p (n t) -> p n t", t=PACK),
+                in0=pre[:].rearrange("p t n -> p n t"),
+                scalar=0.0,
+                in1=lin_sb[:],
+                op0=ALU.max,
+                op1=ALU.mult,
+            )
+
+        z = [keep.tile([P, N // P, CHUNK], F32, name="z%d" % c) for c in range(chunks)]
+
+        def second_layer(c):
+            codes = keep.tile([P, CHUNK], U32, name="codes%d" % c, align_bytes=64)
+            scales = keep.tile([P, CHUNK], U8, name="scales%d" % c, align_bytes=64)
+            nc.vector.quantize_mx(out=codes[:].bitcast(FP8X4), scales=scales[:], in_=hidden[c][:])
+            acc = psum.tile([P, N // P, CHUNK], F32, name="down")
+            for b in range(N // P):
+                nc.tensor.matmul_mx(
+                    out=acc[:, b, :],
+                    lhsT=w2w[:, 2 * P * b : 2 * P * (b + 1)].bitcast(FP4X4),
+                    lhsT_scale=w2_plane[:, P * b : P * (b + 1)],
+                    rhs=codes[:].bitcast(FP8X4),
+                    rhs_scale=scales[:],
+                    start=True,
+                    stop=True,
+                )
+            nc.scalar.copy(out=z[c][:], in_=acc[:])
+
+        def scatter(b, c):
+            nc.vector.tensor_copy(window[b][:].indirect(list_part(c * CHUNK, CHUNK)), z[c][:, b, :])
+
+        per = CHUNK // BLOCK
+        for block in range(S // BLOCK):
+            gate(block)
+            if block < T // BANK:
+                light(0, block)
+            if block % per == 0 and block > 0:
+                second_layer(block // per - 1)
+        second_layer(chunks - 1)
+        for c in range(chunks):
+            light(1, c)
+            scatter(0, c)
+        nc.sync.dma_start(out=out[0:P, :], in_=window[0][:])
+        for c in range(chunks):
+            scatter(1, c)
+        nc.sync.dma_start(out=out[P : 2 * P, :], in_=window[1][:])

@@ -26,7 +26,7 @@ PER_COL = 16
 def load_scale_rows(queue, plane, rows):
     by_quadrant = rows.rearrange("(q r) c -> r q c", r=4)
     for r in range(4):
-        queue.dma_start(out=plane[r:P:32, :].bitcast(I32), in_=by_quadrant[r].bitcast(I32))
+        queue[r].dma_start(out=plane[r:P:32, :].bitcast(I32), in_=by_quadrant[r].bitcast(I32))
 
 
 def tile_moe_cas_glu_relu_kernel(
@@ -36,63 +36,72 @@ def tile_moe_cas_glu_relu_kernel(
     chunks = S // CHUNK
     with ExitStack() as ctx:
         keep = ctx.enter_context(tc.tile_pool(name="keep", bufs=1))
+        reuse = ctx.enter_context(tc.tile_pool(name="reuse", bufs=1))
         ring = ctx.enter_context(tc.tile_pool(name="ring", bufs=3))
         psum = ctx.enter_context(tc.psum_pool(name="psum", bufs=2))
 
+        half = S // 2
         offsets = keep.tile([P, S // PER_COL], U16, name="offsets")
         xw = keep.tile([P, T], I32, name="xw", align_bytes=64)
         xs = keep.tile([P, T], U8, name="xs", align_bytes=64)
-        up_raw = keep.tile([P, 2, 2 * H], U8, name="up_raw", align_bytes=64)
-        up = keep.tile([P, 2 * 2 * H], U8, name="up", align_bytes=64)
-        ws = keep.tile([P, 2 * H + 2 * N], U8, name="ws", align_bytes=64)
+        up = [keep.tile([P, 2 * H], U8, name="up%d" % m, align_bytes=64) for m in range(2)]
         ups = keep.tile([P, 2 * H], U8, name="ups", align_bytes=64)
         ww = keep.tile([P, 2 * N], U8, name="ww", align_bytes=64)
-        w2w = keep.tile([P, 2 * N], U8, name="w2w", align_bytes=64)
 
-        nc.vector.memset(xs[:].bitcast(I32), 0)
-        nc.vector.memset(ws[:].bitcast(I32), 0)
-
-        nc.sync.dma_start(offsets[:], offs)
-        nc.sync.dma_start(out=up_raw[:, 1, :].bitcast(I32), in_=w3_words[0].bitcast(I32))
-        nc.sync.dma_start(out=up_raw[:, 0, :].bitcast(I32), in_=w1_words[0].bitcast(I32))
-        load_scale_rows(nc.scalar, xs, x_scales[0])
-        nc.sync.dma_start(out=xw[:], in_=x_words[0].rearrange("p t d -> p (t d)").bitcast(I32))
-        nc.gpsimd.dma_start(out=ww[:].bitcast(I32), in_=w_words[0].bitcast(I32))
-        nc.gpsimd.dma_start(out=w2w[:].bitcast(I32), in_=w2_words[0].bitcast(I32))
-        load_scale_rows(nc.scalar, ws[:, H : 2 * H], w3_scales[0])
-        load_scale_rows(nc.sync, ws[:, 0:H], w1_scales[0])
-        load_scale_rows(nc.sync, ws[:, 2 * H : 2 * H + N], w_scales[0])
-        load_scale_rows(nc.sync, ws[:, 2 * H + N :], w2_scales[0])
-        w_plane = ws[:, 2 * H : 2 * H + N]
-        w2_plane = ws[:, 2 * H + N :]
+        def shared(name, width, dtype, offset):
+            return reuse.tile([P, width], dtype, name=name, offset=offset, align_bytes=64)
 
         def list_part(first, count):
             return offsets[:, first // PER_COL : (first + count) // PER_COL]
 
-        gs = [keep.tile([P, 2 * CHUNK], U8, name="gs%d" % c, align_bytes=64) for c in range(chunks // 2)]
-        gw = [keep.tile([P, CHUNK], U32, name="gw%d" % c, align_bytes=64) for c in range(chunks)]
-        for c in range(chunks // 2):
-            nc.vector.tensor_copy(gs[c][:], xs[:].indirect(list_part(2 * c * CHUNK, 2 * CHUNK)))
-
-        nc.vector.tensor_copy(
-            out=up[:].bitcast(U16).rearrange("p (w t m) -> p w t m", w=2, t=PACK),
-            in_=up_raw[:].bitcast(U16).rearrange("p w (m t) -> p w t m", t=PACK),
-        )
-        nc.vector.tensor_copy(gw[0][:], xw[:].bitcast(U32).indirect(list_part(0, CHUNK)))
-        for matrix in (1, 0):
-            cols = slice(matrix * H, (matrix + 1) * H)
+        def permute(dst, src):
             nc.vector.tensor_copy(
-                out=ups[:, cols].rearrange("p (t m) -> p t m", t=PACK),
-                in_=ws[:, cols].rearrange("p (m t) -> p t m", t=PACK),
+                out=dst.rearrange("p (t m) -> p t m", t=PACK), in_=src.rearrange("p (m t) -> p t m", t=PACK)
             )
-        for c in range(1, chunks):
-            nc.vector.tensor_copy(gw[c][:], xw[:].bitcast(U32).indirect(list_part(c * CHUNK, CHUNK)))
 
-        window = [keep.tile([P, T], F32, name="window%d" % b) for b in range(N // P)]
+        def gather_words(c, dst):
+            nc.vector.tensor_copy(dst[:], xw[:].bitcast(U32).indirect(list_part(c * CHUNK, CHUNK)))
+            return dst
+
+        def gather_scales(c, dst):
+            nc.vector.tensor_copy(dst[:], xs[:].indirect(list_part(c * half, half)))
+            return dst
+
+        w3_raw = keep.tile([P, 2 * H], U8, name="w3_raw", align_bytes=64)
+        w1_raw = keep.tile([P, 2 * H], U8, name="w1_raw", align_bytes=64)
+        up_rows = shared("up_rows", 2 * H, U8, 512)
+        w_plane = keep.tile([P, N], U8, name="w_plane", align_bytes=64)
+        w2_plane = keep.tile([P, N], U8, name="w2_plane", align_bytes=64)
+        w2w = keep.tile([P, 2 * N], U8, name="w2w", align_bytes=64)
+        nc.gpsimd.dma_start(out=xw[:], in_=x_words[0].rearrange("p t d -> p (t d)").bitcast(I32))
+        nc.gpsimd.dma_start(out=w2w[:].bitcast(I32), in_=w2_words[0].bitcast(I32))
+        nc.sync.dma_start(offsets[:], offs)
+        nc.sync.dma_start(out=w3_raw[:].bitcast(I32), in_=w3_words[0].bitcast(I32))
+        nc.sync.dma_start(out=w1_raw[:].bitcast(I32), in_=w1_words[0].bitcast(I32))
+        nc.sync.dma_start(out=ww[:].bitcast(I32), in_=w_words[0].bitcast(I32))
+        for plane in (xs, w_plane, up_rows, w2_plane):
+            nc.vector.memset(plane[:].bitcast(I32), 0)
+        load_scale_rows([nc.sync] * 4, xs, x_scales[0])
+        load_scale_rows([nc.sync] * 4, w_plane, w_scales[0])
+        load_scale_rows([nc.sync] * 4, up_rows[:, H:], w3_scales[0])
+        load_scale_rows([nc.sync] * 4, up_rows[:, :H], w1_scales[0])
+        load_scale_rows([nc.sync] * 4, w2_plane, w2_scales[0])
+
+        permute(up[1][:].bitcast(U16), w3_raw[:].bitcast(U16))
+        permute(up[0][:].bitcast(U16), w1_raw[:].bitcast(U16))
+        gs = [gather_scales(c, keep.tile([P, half], U8, name="gs%d" % c, align_bytes=64)) for c in range(2)]
+        gw = [gather_words(c, keep.tile([P, CHUNK], U32, name="gw%d" % c, align_bytes=64)) for c in range(chunks - 1)]
+        nc.vector.tensor_copy(
+            out=ups[:].rearrange("p (w t m) -> p w t m", w=2, t=PACK),
+            in_=up_rows[:].rearrange("p (w m t) -> p w t m", w=2, t=PACK),
+        )
+        gw.append(gather_words(chunks - 1, shared("gw_last", CHUNK, U32, -512 + 512)))
+
+        window = [keep.tile([P, T], F32, name="window0"), shared("window1", T, F32, 1024)]
 
         def light(b, j):
             cols = slice(j * BANK, (j + 1) * BANK)
-            acc = psum.tile([P, BANK], F32, name="light")
+            acc = psum.tile([P, BANK], F32, name="light", tag="rows_out")
             nc.tensor.matmul_mx(
                 out=acc[:],
                 lhsT=ww[:, 2 * P * b : 2 * P * (b + 1)].bitcast(FP4X4),
@@ -106,14 +115,14 @@ def tile_moe_cas_glu_relu_kernel(
 
         def first_layer(matrix, block):
             c, lo = divmod(block * BLOCK, CHUNK)
-            c2, lo2 = divmod(block * BLOCK, 2 * CHUNK)
-            acc = psum.tile([P, PACK, BLOCK], F32, name="pre%d" % matrix)
+            c2, lo2 = divmod(block * BLOCK, half)
+            acc = psum.tile([P, PACK, BLOCK], F32, name="pre%d" % matrix, bufs=3)
             for t in range(PACK):
-                col = matrix * H + t * P
+                col = t * P
                 nc.tensor.matmul_mx(
                     out=acc[:, t, :],
-                    lhsT=up[:, 2 * col : 2 * (col + P)].bitcast(FP4X4),
-                    lhsT_scale=ups[:, col : col + P],
+                    lhsT=up[matrix][:, 2 * col : 2 * (col + P)].bitcast(FP4X4),
+                    lhsT_scale=ups[:, matrix * H + col : matrix * H + col + P],
                     rhs=gw[c][:, lo : lo + BLOCK].bitcast(FP8X4),
                     rhs_scale=gs[c2][:, lo2 : lo2 + BLOCK],
                     start=True,
@@ -138,40 +147,43 @@ def tile_moe_cas_glu_relu_kernel(
                 op1=ALU.mult,
             )
 
-        z = [keep.tile([P, N // P, CHUNK], F32, name="z%d" % c) for c in range(chunks)]
+        codes = [keep.tile([P, CHUNK], U32, name="codes%d" % c, align_bytes=64) for c in range(chunks)]
+        scales = [keep.tile([P, CHUNK], U8, name="scales%d" % c, align_bytes=64) for c in range(chunks)]
+        z = {}
 
-        def second_layer(c):
-            codes = keep.tile([P, CHUNK], U32, name="codes%d" % c, align_bytes=64)
-            scales = keep.tile([P, CHUNK], U8, name="scales%d" % c, align_bytes=64)
-            nc.vector.quantize_mx(out=codes[:].bitcast(FP8X4), scales=scales[:], in_=hidden[c][:])
-            acc = psum.tile([P, N // P, CHUNK], F32, name="down")
-            for b in range(N // P):
-                nc.tensor.matmul_mx(
-                    out=acc[:, b, :],
-                    lhsT=w2w[:, 2 * P * b : 2 * P * (b + 1)].bitcast(FP4X4),
-                    lhsT_scale=w2_plane[:, P * b : P * (b + 1)],
-                    rhs=codes[:].bitcast(FP8X4),
-                    rhs_scale=scales[:],
-                    start=True,
-                    stop=True,
-                )
-            nc.scalar.copy(out=z[c][:], in_=acc[:])
+        def quantize(c):
+            nc.vector.quantize_mx(out=codes[c][:].bitcast(FP8X4), scales=scales[c][:], in_=hidden[c][:])
 
-        def scatter(b, c):
-            nc.vector.tensor_copy(window[b][:].indirect(list_part(c * CHUNK, CHUNK)), z[c][:, b, :])
+        def second_layer(b, c):
+            acc = psum.tile([P, CHUNK], F32, name="down", tag="rows_out")
+            nc.tensor.matmul_mx(
+                out=acc[:],
+                lhsT=w2w[:, 2 * P * b : 2 * P * (b + 1)].bitcast(FP4X4),
+                lhsT_scale=w2_plane[:, P * b : P * (b + 1)],
+                rhs=codes[c][:].bitcast(FP8X4),
+                rhs_scale=scales[c][:],
+                start=True,
+                stop=True,
+            )
+            z[b, c] = keep.tile([P, CHUNK], F32, name="z%d_%d" % (b, c))
+            nc.scalar.copy(out=z[b, c][:], in_=acc[:])
+            nc.vector.tensor_copy(window[b][:].indirect(list_part(c * CHUNK, CHUNK)), z[b, c][:])
 
         per = CHUNK // BLOCK
-        for block in range(S // BLOCK):
-            gate(block)
-            if block < T // BANK:
-                light(0, block)
-            if block % per == 0 and block > 0:
-                second_layer(block // per - 1)
-        second_layer(chunks - 1)
+        for j in range(T // BANK):
+            light(0, j)
         for c in range(chunks):
-            light(1, c)
-            scatter(0, c)
+            for block in range(per * c, per * (c + 1)):
+                gate(block)
+            quantize(c)
+            if c == chunks - 1:
+                second_layer(1, 0)
+            second_layer(0, c)
+            if c < chunks - 1:
+                light(1, c)
+            if c == chunks - 2:
+                light(1, c + 1)
         nc.sync.dma_start(out=out[0:P, :], in_=window[0][:])
-        for c in range(chunks):
-            scatter(1, c)
+        for c in range(1, chunks):
+            second_layer(1, c)
         nc.sync.dma_start(out=out[P : 2 * P, :], in_=window[1][:])

@@ -21,6 +21,8 @@ BANK = 512
 BLOCK = 128
 CHUNK = 256
 PER_COL = 16
+ON_VECTOR = 3
+STG = 40960
 
 
 def load_scale_rows(queue, plane, rows):
@@ -37,7 +39,6 @@ def tile_moe_cas_glu_relu_kernel(
     with ExitStack() as ctx:
         keep = ctx.enter_context(tc.tile_pool(name="keep", bufs=1))
         reuse = ctx.enter_context(tc.tile_pool(name="reuse", bufs=1))
-        ring = ctx.enter_context(tc.tile_pool(name="ring", bufs=3))
         psum = ctx.enter_context(tc.psum_pool(name="psum", bufs=2))
 
         half = S // 2
@@ -63,45 +64,51 @@ def tile_moe_cas_glu_relu_kernel(
             nc.vector.tensor_copy(dst[:], xw[:].bitcast(U32).indirect(list_part(c * CHUNK, CHUNK)))
             return dst
 
-        def gather_scales(c, dst):
-            nc.vector.tensor_copy(dst[:], xs[:].indirect(list_part(c * half, half)))
-            return dst
-
         w3_raw = keep.tile([P, 2 * H], U8, name="w3_raw", align_bytes=64)
         w1_raw = keep.tile([P, 2 * H], U8, name="w1_raw", align_bytes=64)
-        up_rows = shared("up_rows", 2 * H, U8, 512)
-        w_plane = keep.tile([P, N], U8, name="w_plane", align_bytes=64)
-        w2_plane = keep.tile([P, N], U8, name="w2_plane", align_bytes=64)
         w2w = keep.tile([P, 2 * N], U8, name="w2w", align_bytes=64)
+        width = 2 * H + 2 * N
+        staged = reuse.tile([16, width], U8, name="staged", offset=STG, align_bytes=64)
         nc.gpsimd.dma_start(out=xw[:], in_=x_words[0].rearrange("p t d -> p (t d)").bitcast(I32))
         nc.gpsimd.dma_start(out=w2w[:].bitcast(I32), in_=w2_words[0].bitcast(I32))
         nc.sync.dma_start(offsets[:], offs)
         nc.sync.dma_start(out=w3_raw[:].bitcast(I32), in_=w3_words[0].bitcast(I32))
         nc.sync.dma_start(out=w1_raw[:].bitcast(I32), in_=w1_words[0].bitcast(I32))
         nc.sync.dma_start(out=ww[:].bitcast(I32), in_=w_words[0].bitcast(I32))
-        for plane in (xs, w_plane, up_rows, w2_plane):
+        lo = 0
+        for source in (w1_scales, w3_scales, w_scales, w2_scales):
+            hi = lo + source.shape[2]
+            nc.scalar.dma_start(out=staged[:, lo:hi].bitcast(I32), in_=source[0].bitcast(I32))
+            lo = hi
+        planes = keep.tile([P, width], U8, name="planes", align_bytes=64)
+        for plane in (xs, planes):
             nc.vector.memset(plane[:].bitcast(I32), 0)
-        load_scale_rows([nc.sync] * 4, xs, x_scales[0])
-        load_scale_rows([nc.sync] * 4, w_plane, w_scales[0])
-        load_scale_rows([nc.sync] * 4, up_rows[:, H:], w3_scales[0])
-        load_scale_rows([nc.sync] * 4, up_rows[:, :H], w1_scales[0])
-        load_scale_rows([nc.sync] * 4, w2_plane, w2_scales[0])
+        load_scale_rows([nc.scalar] * 4, xs, x_scales[0])
+        for r in range(4):
+            nc.sync.dma_start(out=planes[r:P:32, :].bitcast(I32), in_=staged[r:16:4, :].bitcast(I32))
+        w_plane = planes[:, 2 * H : 2 * H + N]
+        w2_plane = planes[:, 2 * H + N :]
 
         permute(up[1][:].bitcast(U16), w3_raw[:].bitcast(U16))
         permute(up[0][:].bitcast(U16), w1_raw[:].bitcast(U16))
-        gs = [gather_scales(c, keep.tile([P, half], U8, name="gs%d" % c, align_bytes=64)) for c in range(2)]
-        gw = [gather_words(c, keep.tile([P, CHUNK], U32, name="gw%d" % c, align_bytes=64)) for c in range(chunks - 1)]
+        def gather_scales(first, count, dst):
+            nc.vector.tensor_copy(dst[:], xs[:].indirect(list_part(first, count)))
+            return [dst[:, lo : lo + CHUNK] for lo in range(0, count, CHUNK)]
+
+        gs = gather_scales(0, CHUNK, keep.tile([P, CHUNK], U8, name="gs0", align_bytes=64))
         nc.vector.tensor_copy(
             out=ups[:].rearrange("p (w t m) -> p w t m", w=2, t=PACK),
-            in_=up_rows[:].rearrange("p (w m t) -> p w t m", w=2, t=PACK),
+            in_=planes[:, : 2 * H].rearrange("p (w m t) -> p w t m", w=2, t=PACK),
         )
-        gw.append(gather_words(chunks - 1, shared("gw_last", CHUNK, U32, -512 + 512)))
+        both = shared("gw01", 2 * CHUNK, U32, STG - 1984)
+        gw = [gather_words(c, both[:, c * CHUNK : (c + 1) * CHUNK]) for c in range(2)]
+        gs.extend(gather_scales(CHUNK, S - CHUNK, shared("gs_rest", S - CHUNK, U8, STG + 64)))
 
-        window = [keep.tile([P, T], F32, name="window0"), shared("window1", T, F32, 1024)]
+        window = [keep.tile([P, T], F32, name="window%d" % b) for b in range(N // P)]
 
         def light(b, j):
             cols = slice(j * BANK, (j + 1) * BANK)
-            acc = psum.tile([P, BANK], F32, name="light", tag="rows_out")
+            acc = psum.tile([P, BANK], F32, name="light", tag="rows_out", bufs=4)
             nc.tensor.matmul_mx(
                 out=acc[:],
                 lhsT=ww[:, 2 * P * b : 2 * P * (b + 1)].bitcast(FP4X4),
@@ -115,8 +122,7 @@ def tile_moe_cas_glu_relu_kernel(
 
         def first_layer(matrix, block):
             c, lo = divmod(block * BLOCK, CHUNK)
-            c2, lo2 = divmod(block * BLOCK, half)
-            acc = psum.tile([P, PACK, BLOCK], F32, name="pre%d" % matrix, bufs=3)
+            acc = psum.tile([P, PACK, BLOCK], F32, name="pre%d" % matrix, bufs=2)
             for t in range(PACK):
                 col = t * P
                 nc.tensor.matmul_mx(
@@ -124,28 +130,39 @@ def tile_moe_cas_glu_relu_kernel(
                     lhsT=up[matrix][:, 2 * col : 2 * (col + P)].bitcast(FP4X4),
                     lhsT_scale=ups[:, matrix * H + col : matrix * H + col + P],
                     rhs=gw[c][:, lo : lo + BLOCK].bitcast(FP8X4),
-                    rhs_scale=gs[c2][:, lo2 : lo2 + BLOCK],
+                    rhs_scale=gs[c][:, lo : lo + BLOCK],
                     start=True,
                     stop=True,
                 )
             return acc
 
-        hidden = [keep.tile([P, CHUNK * PACK], BF16, name="hidden%d" % c, align_bytes=64) for c in range(chunks)]
+        hidden = [shared("hidden%d" % c, CHUNK * PACK, BF16, 2048 * (1 + c)) for c in range(chunks)]
+        stage_at = 2048 * (1 + chunks)
 
         def gate(block):
             c, lo = divmod(block * BLOCK, CHUNK)
+            dst = hidden[c][:, lo * PACK : (lo + BLOCK) * PACK]
             lin = first_layer(1, block)
-            lin_sb = ring.tile([P, BLOCK, PACK], F32, name="lin_sb")
-            nc.scalar.copy(out=lin_sb[:], in_=lin[:].rearrange("p t n -> p n t"))
+            lin_sb = shared("lin_sb%d" % block, BANK, F32, stage_at + 2048 * block)
+            nc.scalar.copy(out=lin_sb[:].rearrange("p (n t) -> p n t", t=PACK), in_=lin[:].rearrange("p t n -> p n t"))
             pre = first_layer(0, block)
-            nc.vector.scalar_tensor_tensor(
-                out=hidden[c][:, lo * PACK : (lo + BLOCK) * PACK].rearrange("p (n t) -> p n t", t=PACK),
-                in0=pre[:].rearrange("p t n -> p n t"),
-                scalar=0.0,
-                in1=lin_sb[:],
-                op0=ALU.max,
-                op1=ALU.mult,
-            )
+            if block < ON_VECTOR:
+                nc.vector.scalar_tensor_tensor(
+                    out=dst.rearrange("p (n t) -> p n t", t=PACK),
+                    in0=pre[:].rearrange("p t n -> p n t"),
+                    scalar=0.0,
+                    in1=lin_sb[:].rearrange("p (n t) -> p n t", t=PACK),
+                    op0=ALU.max,
+                    op1=ALU.mult,
+                )
+            else:
+                act_sb = keep.tile([P, BANK], F32, name="act_sb%d" % block)
+                nc.scalar.activation(
+                    out=act_sb[:].rearrange("p (n t) -> p n t", t=PACK),
+                    in_=pre[:].rearrange("p t n -> p n t"),
+                    func=mybir.ActivationFunctionType.Relu,
+                )
+                nc.gpsimd.tensor_tensor(out=dst, in0=act_sb[:], in1=lin_sb[:], op=ALU.mult)
 
         codes = [keep.tile([P, CHUNK], U32, name="codes%d" % c, align_bytes=64) for c in range(chunks)]
         scales = [keep.tile([P, CHUNK], U8, name="scales%d" % c, align_bytes=64) for c in range(chunks)]
@@ -155,7 +172,7 @@ def tile_moe_cas_glu_relu_kernel(
             nc.vector.quantize_mx(out=codes[c][:].bitcast(FP8X4), scales=scales[c][:], in_=hidden[c][:])
 
         def second_layer(b, c):
-            acc = psum.tile([P, CHUNK], F32, name="down", tag="rows_out")
+            acc = psum.tile([P, CHUNK], F32, name="down", tag="rows_out", bufs=4)
             nc.tensor.matmul_mx(
                 out=acc[:],
                 lhsT=w2w[:, 2 * P * b : 2 * P * (b + 1)].bitcast(FP4X4),
@@ -165,25 +182,35 @@ def tile_moe_cas_glu_relu_kernel(
                 start=True,
                 stop=True,
             )
-            z[b, c] = keep.tile([P, CHUNK], F32, name="z%d_%d" % (b, c))
+            if b == 1 and c < chunks - 1:
+                z[b, c] = shared("z%d_%d" % (b, c), CHUNK, F32, stage_at + 2048 * (2 * c + 3))
+            else:
+                z[b, c] = keep.tile([P, CHUNK], F32, name="z%d_%d" % (b, c))
             nc.scalar.copy(out=z[b, c][:], in_=acc[:])
             nc.vector.tensor_copy(window[b][:].indirect(list_part(c * CHUNK, CHUNK)), z[b, c][:])
 
-        per = CHUNK // BLOCK
-        for j in range(T // BANK):
-            light(0, j)
-        for c in range(chunks):
-            for block in range(per * c, per * (c + 1)):
-                gate(block)
+        lights = [(b, j) for b in range(N // P) for j in range(T // BANK)]
+        for b, j in lights[:4]:
+            light(b, j)
+        for c in range(2):
+            gate(2 * c)
+            gate(2 * c + 1)
             quantize(c)
-            if c == chunks - 1:
-                second_layer(1, 0)
+            if c == 0:
+                rest = shared("gw23", 2 * CHUNK, U32, stage_at + 2048)
+                gw.extend([gather_words(d, rest[:, (d - 2) * CHUNK : (d - 1) * CHUNK]) for d in (2, 3)])
+                for b, j in lights[4:]:
+                    light(b, j)
+        second_layer(0, 0)
+        second_layer(1, 0)
+        for c in range(2, chunks):
+            gate(2 * c)
+            if c == 2:
+                second_layer(0, 1)
+            gate(2 * c + 1)
+            quantize(c)
+            second_layer(1, c - 1)
             second_layer(0, c)
-            if c < chunks - 1:
-                light(1, c)
-            if c == chunks - 2:
-                light(1, c + 1)
         nc.sync.dma_start(out=out[0:P, :], in_=window[0][:])
-        for c in range(1, chunks):
-            second_layer(1, c)
+        second_layer(1, chunks - 1)
         nc.sync.dma_start(out=out[P : 2 * P, :], in_=window[1][:])

@@ -136,7 +136,7 @@ def tile_moe_cas_glu_relu_kernel(
                 )
             return acc
 
-        hidden = [shared("hidden%d" % c, CHUNK * PACK, BF16, 2048 * (1 + c)) for c in range(chunks)]
+        hidden = [shared("hidden%d" % c, CHUNK * PACK, BF16, 2048) for c in range(chunks)]
         stage_at = 2048 * (1 + chunks)
 
         def gate(block):
@@ -199,15 +199,17 @@ def tile_moe_cas_glu_relu_kernel(
             if c == 0:
                 rest = shared("gw23", 2 * CHUNK, U32, stage_at + 2048)
                 gw.extend([gather_words(d, rest[:, (d - 2) * CHUNK : (d - 1) * CHUNK]) for d in (2, 3)])
-                for b, j in lights[4:]:
+                for b, j in lights[4:6]:
                     light(b, j)
         second_layer(0, 0)
+        for b, j in lights[6:]:
+            light(b, j)
         second_layer(1, 0)
         for c in range(2, chunks):
             gate(2 * c)
+            gate(2 * c + 1)
             if c == 2:
                 second_layer(0, 1)
-            gate(2 * c + 1)
             quantize(c)
             second_layer(1, c - 1)
             second_layer(0, c)

@@ -21,7 +21,7 @@ BANK = 512
 BLOCK = 128
 CHUNK = 256
 PER_COL = 16
-ON_VECTOR = 3
+ON_VECTOR = 4
 STG = 40960
 
 
@@ -67,42 +67,44 @@ def tile_moe_cas_glu_relu_kernel(
         w3_raw = keep.tile([P, 2 * H], U8, name="w3_raw", align_bytes=64)
         w1_raw = keep.tile([P, 2 * H], U8, name="w1_raw", align_bytes=64)
         w2w = keep.tile([P, 2 * N], U8, name="w2w", align_bytes=64)
-        width = 2 * H + 2 * N
+        width = 2 * H + N
         staged = reuse.tile([16, width], U8, name="staged", offset=STG, align_bytes=64)
-        nc.gpsimd.dma_start(out=xw[:], in_=x_words[0].rearrange("p t d -> p (t d)").bitcast(I32))
-        nc.gpsimd.dma_start(out=w2w[:].bitcast(I32), in_=w2_words[0].bitcast(I32))
-        nc.sync.dma_start(offsets[:], offs)
-        nc.sync.dma_start(out=w3_raw[:].bitcast(I32), in_=w3_words[0].bitcast(I32))
-        nc.sync.dma_start(out=w1_raw[:].bitcast(I32), in_=w1_words[0].bitcast(I32))
-        nc.sync.dma_start(out=ww[:].bitcast(I32), in_=w_words[0].bitcast(I32))
-        lo = 0
-        for source in (w1_scales, w3_scales, w_scales, w2_scales):
-            hi = lo + source.shape[2]
-            nc.scalar.dma_start(out=staged[:, lo:hi].bitcast(I32), in_=source[0].bitcast(I32))
-            lo = hi
         planes = keep.tile([P, width], U8, name="planes", align_bytes=64)
         for plane in (xs, planes):
             nc.vector.memset(plane[:].bitcast(I32), 0)
-        load_scale_rows([nc.scalar] * 4, xs, x_scales[0])
+        nc.gpsimd.dma_start(out=xw[:], in_=x_words[0].rearrange("p t d -> p (t d)").bitcast(I32))
+        nc.gpsimd.dma_start(out=w2w[:].bitcast(I32), in_=w2_words[0].bitcast(I32))
+        nc.sync.dma_start(offsets[:], offs)
+        load_scale_rows([nc.sync, nc.scalar] * 2, xs, x_scales[0])
+        lo = 0
+        for queue, source in ((nc.scalar, w1_scales), (nc.sync, w3_scales), (nc.scalar, w_scales)):
+            hi = lo + source.shape[2]
+            queue.dma_start(out=staged[:, lo:hi].bitcast(I32), in_=source[0].bitcast(I32))
+            lo = hi
+        nc.sync.dma_start(out=w3_raw[:].bitcast(I32), in_=w3_words[0].bitcast(I32))
+        nc.sync.dma_start(out=w1_raw[:].bitcast(I32), in_=w1_words[0].bitcast(I32))
+        nc.sync.dma_start(out=ww[:].bitcast(I32), in_=w_words[0].bitcast(I32))
         for r in range(4):
             nc.sync.dma_start(out=planes[r:P:32, :].bitcast(I32), in_=staged[r:16:4, :].bitcast(I32))
-        w_plane = planes[:, 2 * H : 2 * H + N]
-        w2_plane = planes[:, 2 * H + N :]
+        w_plane = planes[:, 2 * H :]
 
-        permute(up[1][:].bitcast(U16), w3_raw[:].bitcast(U16))
-        permute(up[0][:].bitcast(U16), w1_raw[:].bitcast(U16))
         def gather_scales(first, count, dst):
             nc.vector.tensor_copy(dst[:], xs[:].indirect(list_part(first, count)))
             return [dst[:, lo : lo + CHUNK] for lo in range(0, count, CHUNK)]
 
-        gs = gather_scales(0, CHUNK, keep.tile([P, CHUNK], U8, name="gs0", align_bytes=64))
+        gs = gather_scales(0, S, keep.tile([P, S], U8, name="gs", align_bytes=64))
+        permute(up[1][:].bitcast(U16), w3_raw[:].bitcast(U16))
+        permute(up[0][:].bitcast(U16), w1_raw[:].bitcast(U16))
+        gw = [gather_words(0, keep.tile([P, CHUNK], U32, name="gw0", align_bytes=64))]
         nc.vector.tensor_copy(
             out=ups[:].rearrange("p (w t m) -> p w t m", w=2, t=PACK),
             in_=planes[:, : 2 * H].rearrange("p (w m t) -> p w t m", w=2, t=PACK),
         )
-        both = shared("gw01", 2 * CHUNK, U32, STG - 1984)
-        gw = [gather_words(c, both[:, c * CHUNK : (c + 1) * CHUNK]) for c in range(2)]
-        gs.extend(gather_scales(CHUNK, S - CHUNK, shared("gs_rest", S - CHUNK, U8, STG + 64)))
+        w2_plane = shared("w2_plane", N, U8, STG)
+        nc.vector.memset(w2_plane[:].bitcast(I32), 0)
+        load_scale_rows([nc.sync] * 4, w2_plane, w2_scales[0])
+        rest = shared("gw_rest", S - CHUNK, U32, STG + N)
+        gw.extend([gather_words(c, rest[:, (c - 1) * CHUNK : c * CHUNK]) for c in range(1, chunks)])
 
         window = [keep.tile([P, T], F32, name="window%d" % b) for b in range(N // P)]
 
@@ -197,8 +199,6 @@ def tile_moe_cas_glu_relu_kernel(
             gate(2 * c + 1)
             quantize(c)
             if c == 0:
-                rest = shared("gw23", 2 * CHUNK, U32, stage_at + 2048)
-                gw.extend([gather_words(d, rest[:, (d - 2) * CHUNK : (d - 1) * CHUNK]) for d in (2, 3)])
                 for b, j in lights[4:6]:
                     light(b, j)
         second_layer(0, 0)

@@ -14,21 +14,28 @@ U8 = mybir.dt.uint8
 FP8X4 = mybir.dt.float8_e4m3fn_x4
 FP4X4 = mybir.dt.float4_e2m1fn_x4
 ALU = mybir.AluOpType
+ACT = mybir.ActivationFunctionType
 
 P = 128
 PACK = 4
 BANK = 512
+BANK_BYTES = 2048
 BLOCK = 128
 CHUNK = 256
 PER_COL = 16
-ON_VECTOR = 4
-STG = 40960
+W1, W3 = 0, 1
+RAW3 = 4096
+SCALES0 = 8192
+CODES0 = SCALES0 + BANK_BYTES
+HIDDEN = CODES0 + BANK_BYTES
+ACT5 = HIDDEN + BANK_BYTES
+ACT7 = ACT5 + BANK_BYTES
 
 
-def load_scale_rows(queue, plane, rows):
+def load_scale_rows(queues, plane, rows):
     by_quadrant = rows.rearrange("(q r) c -> r q c", r=4)
     for r in range(4):
-        queue[r].dma_start(out=plane[r:P:32, :].bitcast(I32), in_=by_quadrant[r].bitcast(I32))
+        queues[r].dma_start(out=plane[r:P:32, :].bitcast(I32), in_=by_quadrant[r].bitcast(I32))
 
 
 def tile_moe_cas_glu_relu_kernel(
@@ -39,78 +46,76 @@ def tile_moe_cas_glu_relu_kernel(
     with ExitStack() as ctx:
         keep = ctx.enter_context(tc.tile_pool(name="keep", bufs=1))
         reuse = ctx.enter_context(tc.tile_pool(name="reuse", bufs=1))
-        psum = ctx.enter_context(tc.psum_pool(name="psum", bufs=2))
+        psum = ctx.enter_context(tc.psum_pool(name="psum", bufs=1))
 
-        half = S // 2
-        offsets = keep.tile([P, S // PER_COL], U16, name="offsets")
-        xw = keep.tile([P, T], I32, name="xw", align_bytes=64)
-        xs = keep.tile([P, T], U8, name="xs", align_bytes=64)
-        up = [keep.tile([P, 2 * H], U8, name="up%d" % m, align_bytes=64) for m in range(2)]
-        ups = keep.tile([P, 2 * H], U8, name="ups", align_bytes=64)
-        ww = keep.tile([P, 2 * N], U8, name="ww", align_bytes=64)
+        def kept(name, width, dtype):
+            return keep.tile([P, width], dtype, name=name, align_bytes=64)
 
         def shared(name, width, dtype, offset):
             return reuse.tile([P, width], dtype, name=name, offset=offset, align_bytes=64)
 
+        def bank(name, shape, index):
+            return psum.tile(shape, F32, name=name, offset=index * BANK_BYTES)
+
+        offsets = keep.tile([P, S // PER_COL], U16, name="offsets")
+        xw = kept("xw", T, I32)
+        xs = kept("xs", T, U8)
+        ww = kept("ww", 2 * N, U8)
+        w2w = kept("w2w", 2 * N, U8)
+        w2_plane = kept("w2_plane", N, U8)
+        width = 2 * H + N
+        staged = keep.tile([16, width], U8, name="staged", align_bytes=64)
+        planes = kept("planes", width, U8)
+        raw = [shared("raw%d" % m, 2 * H, U8, at) for m, at in ((W1, RAW3), (W3, 0))]
+        up = [kept("up%d" % m, 2 * H, U8) for m in (W1, W3)]
+
         def list_part(first, count):
             return offsets[:, first // PER_COL : (first + count) // PER_COL]
 
-        def permute(dst, src):
-            nc.vector.tensor_copy(
-                out=dst.rearrange("p (t m) -> p t m", t=PACK), in_=src.rearrange("p (m t) -> p t m", t=PACK)
-            )
-
-        def gather_words(c, dst):
-            nc.vector.tensor_copy(dst[:], xw[:].bitcast(U32).indirect(list_part(c * CHUNK, CHUNK)))
-            return dst
-
-        w3_raw = keep.tile([P, 2 * H], U8, name="w3_raw", align_bytes=64)
-        w1_raw = keep.tile([P, 2 * H], U8, name="w1_raw", align_bytes=64)
-        w2w = keep.tile([P, 2 * N], U8, name="w2w", align_bytes=64)
-        width = 2 * H + N
-        staged = reuse.tile([16, width], U8, name="staged", offset=STG, align_bytes=64)
-        planes = keep.tile([P, width], U8, name="planes", align_bytes=64)
-        for plane in (xs, planes):
+        for plane in (xs, w2_plane):
             nc.vector.memset(plane[:].bitcast(I32), 0)
-        nc.gpsimd.dma_start(out=xw[:], in_=x_words[0].rearrange("p t d -> p (t d)").bitcast(I32))
-        nc.gpsimd.dma_start(out=w2w[:].bitcast(I32), in_=w2_words[0].bitcast(I32))
+        words = x_words[0].rearrange("p t d -> p (t d)").bitcast(I32)
+        nc.gpsimd.dma_start(out=xw[:, : T // 2], in_=words[:, : T // 2])
+        nc.gpsimd.memset(planes[:].bitcast(I32), 0)
+        nc.gpsimd.dma_start(out=xw[:, T // 2 :], in_=words[:, T // 2 :])
         nc.sync.dma_start(offsets[:], offs)
-        load_scale_rows([nc.sync, nc.scalar] * 2, xs, x_scales[0])
         lo = 0
         for queue, source in ((nc.scalar, w1_scales), (nc.sync, w3_scales), (nc.scalar, w_scales)):
             hi = lo + source.shape[2]
             queue.dma_start(out=staged[:, lo:hi].bitcast(I32), in_=source[0].bitcast(I32))
             lo = hi
-        nc.sync.dma_start(out=w3_raw[:].bitcast(I32), in_=w3_words[0].bitcast(I32))
-        nc.sync.dma_start(out=w1_raw[:].bitcast(I32), in_=w1_words[0].bitcast(I32))
-        nc.sync.dma_start(out=ww[:].bitcast(I32), in_=w_words[0].bitcast(I32))
-        for r in range(4):
-            nc.sync.dma_start(out=planes[r:P:32, :].bitcast(I32), in_=staged[r:16:4, :].bitcast(I32))
+        load_scale_rows([nc.sync, nc.scalar] * 2, xs, x_scales[0])
+        nc.sync.dma_start(out=raw[W3][:].bitcast(I32), in_=w3_words[0].bitcast(I32))
+        nc.scalar.dma_start(out=ww[:].bitcast(I32), in_=w_words[0].bitcast(I32))
+        for r, queue in enumerate([nc.sync, nc.scalar] * 2):
+            queue.dma_start(out=planes[r:P:32, :].bitcast(I32), in_=staged[r:16:4, :].bitcast(I32))
+        nc.sync.dma_start(out=raw[W1][:].bitcast(I32), in_=w1_words[0].bitcast(I32))
+        nc.sync.dma_start(out=w2w[:].bitcast(I32), in_=w2_words[0].bitcast(I32))
+        load_scale_rows([nc.sync] * 4, w2_plane, w2_scales[0])
         w_plane = planes[:, 2 * H :]
 
-        def gather_scales(first, count, dst):
-            nc.vector.tensor_copy(dst[:], xs[:].indirect(list_part(first, count)))
-            return [dst[:, lo : lo + CHUNK] for lo in range(0, count, CHUNK)]
+        gs = kept("gs", S, U8)
+        nc.vector.tensor_copy(gs[:], xs[:].indirect(offsets[:]))
+        for m in (W3, W1):
+            nc.vector.tensor_copy(
+                out=up[m][:].bitcast(U16).rearrange("p (t m) -> p t m", t=PACK),
+                in_=raw[m][:].bitcast(U16).rearrange("p (m t) -> p t m", t=PACK),
+            )
+        gw = shared("gw", S, U32, RAW3 + H - 4 * S)
+        nc.vector.tensor_copy(gw[:, :CHUNK], xw[:].bitcast(U32).indirect(list_part(0, CHUNK)))
+        ups = shared("ups", 2 * H, U8, RAW3 + H)
+        for m in (W3, W1):
+            nc.gpsimd.tensor_copy(
+                out=ups[:, m * H : (m + 1) * H].rearrange("p (t m) -> p t m", t=PACK),
+                in_=planes[:, m * H : (m + 1) * H].rearrange("p (m t) -> p t m", t=PACK),
+            )
+        nc.vector.tensor_copy(gw[:, CHUNK:], xw[:].bitcast(U32).indirect(list_part(CHUNK, S - CHUNK)))
 
-        gs = gather_scales(0, S, keep.tile([P, S], U8, name="gs", align_bytes=64))
-        permute(up[1][:].bitcast(U16), w3_raw[:].bitcast(U16))
-        permute(up[0][:].bitcast(U16), w1_raw[:].bitcast(U16))
-        gw = [gather_words(0, keep.tile([P, CHUNK], U32, name="gw0", align_bytes=64))]
-        nc.vector.tensor_copy(
-            out=ups[:].rearrange("p (w t m) -> p w t m", w=2, t=PACK),
-            in_=planes[:, : 2 * H].rearrange("p (w m t) -> p w t m", w=2, t=PACK),
-        )
-        w2_plane = shared("w2_plane", N, U8, STG)
-        nc.vector.memset(w2_plane[:].bitcast(I32), 0)
-        load_scale_rows([nc.sync] * 4, w2_plane, w2_scales[0])
-        rest = shared("gw_rest", S - CHUNK, U32, STG + N)
-        gw.extend([gather_words(c, rest[:, (c - 1) * CHUNK : c * CHUNK]) for c in range(1, chunks)])
+        window = [kept("window0", T, F32), kept("window1", T, F32)]
 
-        window = [keep.tile([P, T], F32, name="window%d" % b) for b in range(N // P)]
-
-        def light(b, j):
+        def light(b, j, index):
             cols = slice(j * BANK, (j + 1) * BANK)
-            acc = psum.tile([P, BANK], F32, name="light", tag="rows_out", bufs=4)
+            acc = bank("light%d_%d" % (b, j), [P, BANK], index)
             nc.tensor.matmul_mx(
                 out=acc[:],
                 lhsT=ww[:, 2 * P * b : 2 * P * (b + 1)].bitcast(FP4X4),
@@ -122,97 +127,127 @@ def tile_moe_cas_glu_relu_kernel(
             )
             nc.scalar.copy(out=window[b][:, cols], in_=acc[:])
 
-        def first_layer(matrix, block):
-            c, lo = divmod(block * BLOCK, CHUNK)
-            acc = psum.tile([P, PACK, BLOCK], F32, name="pre%d" % matrix, bufs=2)
+        def first_layer(matrix, block, index):
+            acc = bank("pre%d_%d" % (matrix, block), [P, PACK, BLOCK], index)
             for t in range(PACK):
                 col = t * P
                 nc.tensor.matmul_mx(
                     out=acc[:, t, :],
                     lhsT=up[matrix][:, 2 * col : 2 * (col + P)].bitcast(FP4X4),
                     lhsT_scale=ups[:, matrix * H + col : matrix * H + col + P],
-                    rhs=gw[c][:, lo : lo + BLOCK].bitcast(FP8X4),
-                    rhs_scale=gs[c][:, lo : lo + BLOCK],
+                    rhs=gw[:, block * BLOCK : (block + 1) * BLOCK].bitcast(FP8X4),
+                    rhs_scale=gs[:, block * BLOCK : (block + 1) * BLOCK],
+                    start=True,
+                    stop=True,
+                )
+            return acc[:].rearrange("p t n -> p n t")
+
+        hidden = [kept("hidden%d" % c, CHUNK * PACK, BF16) for c in range(1)]
+        hidden.extend([shared("hidden%d" % c, CHUNK * PACK, BF16, HIDDEN) for c in range(1, chunks)])
+        lin_sb = {}
+
+        def by_token(ap):
+            return ap.rearrange("p (n t) -> p n t", t=PACK)
+
+        def hidden_part(block):
+            c, lo = divmod(block * BLOCK, CHUNK)
+            return hidden[c][:, lo * PACK : (lo + BLOCK) * PACK]
+
+        lin_at = {3: SCALES0}
+
+        def linear(block, index):
+            if block in lin_at:
+                lin_sb[block] = shared("lin_sb%d" % block, BANK, F32, lin_at[block])
+            else:
+                lin_sb[block] = kept("lin_sb%d" % block, BANK, F32)
+            nc.scalar.copy(out=by_token(lin_sb[block][:]), in_=first_layer(W3, block, index))
+
+        def gate_on_vector(block, index):
+            nc.vector.scalar_tensor_tensor(
+                out=by_token(hidden_part(block)),
+                in0=first_layer(W1, block, index),
+                scalar=0.0,
+                in1=by_token(lin_sb[block][:]),
+                op0=ALU.max,
+                op1=ALU.mult,
+            )
+
+        def gate_on_gpsimd(block, index, act_sb):
+            nc.scalar.activation(out=by_token(act_sb[:]), in_=first_layer(W1, block, index), func=ACT.Relu)
+            nc.gpsimd.tensor_tensor(out=hidden_part(block), in0=act_sb[:], in1=lin_sb[block][:], op=ALU.mult)
+
+        codes = [shared("codes%d" % c, CHUNK, U32, at) for c, at in enumerate((CODES0,))]
+        codes.extend([kept("codes%d" % c, CHUNK, U32) for c in range(1, chunks)])
+        scales = [shared("scales%d" % c, CHUNK, U8, at) for c, at in enumerate((SCALES0,))]
+        scales.extend([kept("scales%d" % c, CHUNK, U8) for c in range(1, chunks)])
+
+        def quantize(c):
+            nc.vector.quantize_mx(out=codes[c][:].bitcast(FP8X4), scales=scales[c][:], in_=hidden[c][:])
+
+        def second_layer(c, index, blocks=(0, 1)):
+            acc = bank("down%d_%d" % (c, blocks[0]), [P, len(blocks) * CHUNK], index)
+            for at, b in enumerate(blocks):
+                nc.tensor.matmul_mx(
+                    out=acc[:, at * CHUNK : (at + 1) * CHUNK],
+                    lhsT=w2w[:, 2 * P * b : 2 * P * (b + 1)].bitcast(FP4X4),
+                    lhsT_scale=w2_plane[:, P * b : P * (b + 1)],
+                    rhs=codes[c][:].bitcast(FP8X4),
+                    rhs_scale=scales[c][:],
                     start=True,
                     stop=True,
                 )
             return acc
 
-        hidden = [shared("hidden%d" % c, CHUNK * PACK, BF16, 2048) for c in range(chunks)]
-        stage_at = 2048 * (1 + chunks)
+        def scatter(b, c, z):
+            nc.vector.tensor_copy(window[b][:].indirect(list_part(c * CHUNK, z.shape[1])), z)
 
-        def gate(block):
-            c, lo = divmod(block * BLOCK, CHUNK)
-            dst = hidden[c][:, lo * PACK : (lo + BLOCK) * PACK]
-            lin = first_layer(1, block)
-            lin_sb = shared("lin_sb%d" % block, BANK, F32, stage_at + 2048 * block)
-            nc.scalar.copy(out=lin_sb[:].rearrange("p (n t) -> p n t", t=PACK), in_=lin[:].rearrange("p t n -> p n t"))
-            pre = first_layer(0, block)
-            if block < ON_VECTOR:
-                nc.vector.scalar_tensor_tensor(
-                    out=dst.rearrange("p (n t) -> p n t", t=PACK),
-                    in0=pre[:].rearrange("p t n -> p n t"),
-                    scalar=0.0,
-                    in1=lin_sb[:].rearrange("p (n t) -> p n t", t=PACK),
-                    op0=ALU.max,
-                    op1=ALU.mult,
-                )
-            else:
-                act_sb = keep.tile([P, BANK], F32, name="act_sb%d" % block)
-                nc.scalar.activation(
-                    out=act_sb[:].rearrange("p (n t) -> p n t", t=PACK),
-                    in_=pre[:].rearrange("p t n -> p n t"),
-                    func=mybir.ActivationFunctionType.Relu,
-                )
-                nc.gpsimd.tensor_tensor(out=dst, in0=act_sb[:], in1=lin_sb[:], op=ALU.mult)
+        def bring(acc, b, c, z):
+            nc.scalar.copy(out=z[:], in_=acc)
+            scatter(b, c, z[:])
 
-        codes = [keep.tile([P, CHUNK], U32, name="codes%d" % c, align_bytes=64) for c in range(chunks)]
-        scales = [keep.tile([P, CHUNK], U8, name="scales%d" % c, align_bytes=64) for c in range(chunks)]
-        z = {}
-
-        def quantize(c):
-            nc.vector.quantize_mx(out=codes[c][:].bitcast(FP8X4), scales=scales[c][:], in_=hidden[c][:])
-
-        def second_layer(b, c):
-            acc = psum.tile([P, CHUNK], F32, name="down", tag="rows_out", bufs=4)
-            nc.tensor.matmul_mx(
-                out=acc[:],
-                lhsT=w2w[:, 2 * P * b : 2 * P * (b + 1)].bitcast(FP4X4),
-                lhsT_scale=w2_plane[:, P * b : P * (b + 1)],
-                rhs=codes[c][:].bitcast(FP8X4),
-                rhs_scale=scales[c][:],
-                start=True,
-                stop=True,
-            )
-            if b == 1 and c < chunks - 1:
-                z[b, c] = shared("z%d_%d" % (b, c), CHUNK, F32, stage_at + 2048 * (2 * c + 3))
-            else:
-                z[b, c] = keep.tile([P, CHUNK], F32, name="z%d_%d" % (b, c))
-            nc.scalar.copy(out=z[b, c][:], in_=acc[:])
-            nc.vector.tensor_copy(window[b][:].indirect(list_part(c * CHUNK, CHUNK)), z[b, c][:])
-
-        lights = [(b, j) for b in range(N // P) for j in range(T // BANK)]
-        for b, j in lights[:4]:
-            light(b, j)
-        for c in range(2):
-            gate(2 * c)
-            gate(2 * c + 1)
-            quantize(c)
-            if c == 0:
-                for b, j in lights[4:6]:
-                    light(b, j)
-        second_layer(0, 0)
-        for b, j in lights[6:]:
-            light(b, j)
-        second_layer(1, 0)
-        for c in range(2, chunks):
-            gate(2 * c)
-            gate(2 * c + 1)
-            if c == 2:
-                second_layer(0, 1)
-            quantize(c)
-            second_layer(1, c - 1)
-            second_layer(0, c)
+        for index, (b, j) in enumerate(((0, 0), (0, 1), (1, 0), (1, 1))):
+            light(b, j, index)
+        linear(0, 4)
+        gate_on_vector(0, 5)
+        linear(1, 6)
+        gate_on_vector(1, 7)
+        quantize(0)
+        light(0, 2, 4)
+        linear(2, 5)
+        gate_on_vector(2, 7)
+        light(0, 3, 6)
+        down00 = second_layer(0, 0, (0,))
+        down10 = second_layer(0, 1, (1,))
+        z00 = kept("z0_0", CHUNK, F32)
+        bring(down00[:], 0, 0, z00)
+        z10 = shared("z1_0", CHUNK, F32, CODES0)
+        nc.scalar.copy(out=z10[:], in_=down10[:])
+        linear(3, 4)
+        gate_on_vector(3, 7)
+        quantize(1)
+        light(1, 2, 0)
+        light(1, 3, 1)
+        scatter(1, 0, z10[:])
+        linear(4, 4)
+        gate_on_gpsimd(4, 0, kept("act_sb4", BANK, F32))
+        linear(5, 1)
+        down1 = second_layer(1, 2)
+        bring(down1[:, :CHUNK], 0, 1, kept("z0_1", CHUNK, F32))
+        gate_on_gpsimd(5, 4, shared("act_sb5", BANK, F32, ACT5))
+        quantize(2)
+        linear(6, 0)
+        gate_on_gpsimd(6, 1, kept("act_sb6", BANK, F32))
+        linear(7, 4)
+        bring(down1[:, CHUNK:], 1, 1, shared("z1_1", CHUNK, F32, ACT5))
+        gate_on_gpsimd(7, 0, shared("act_sb7", BANK, F32, ACT7))
+        down2 = second_layer(2, 3)
+        bring(down2[:, :CHUNK], 0, 2, kept("z0_2", CHUNK, F32))
+        quantize(3)
+        bring(down2[:, CHUNK:], 1, 2, shared("z1_2", CHUNK, F32, ACT7))
+        down3 = second_layer(3, 5)
+        last = kept("z_last", 2 * CHUNK, F32)
+        nc.scalar.copy(out=last[:], in_=down3[:])
+        scatter(0, 3, last[:, :CHUNK])
         nc.sync.dma_start(out=out[0:P, :], in_=window[0][:])
-        second_layer(1, chunks - 1)
+        scatter(1, 3, last[:, CHUNK:])
         nc.sync.dma_start(out=out[P : 2 * P, :], in_=window[1][:])

@@ -23,13 +23,16 @@ BANK_BYTES = 2048
 BLOCK = 128
 CHUNK = 256
 PER_COL = 16
+FILL = 192
 W1, W3 = 0, 1
 RAW3 = 4096
-SCALES0 = 8192
-CODES0 = SCALES0 + BANK_BYTES
-HIDDEN = CODES0 + BANK_BYTES
-ACT5 = HIDDEN + BANK_BYTES
-ACT7 = ACT5 + BANK_BYTES
+LIN5 = 8192
+LIN6 = LIN5 + BANK_BYTES
+CODES1 = LIN6 - 512
+SCALES1 = LIN6 + BANK_BYTES
+HIDDEN = SCALES1 + BANK_BYTES
+ACT5 = SCALES1
+ACT7 = HIDDEN + BANK_BYTES
 
 
 def load_scale_rows(queues, plane, rows):
@@ -94,6 +97,8 @@ def tile_moe_cas_glu_relu_kernel(
         load_scale_rows([nc.sync] * 4, w2_plane, w2_scales[0])
         w_plane = planes[:, 2 * H :]
 
+        zeros = kept("zeros", FILL, F32)
+        nc.vector.memset(zeros[:], 0.0)
         gs = kept("gs", S, U8)
         nc.vector.tensor_copy(gs[:], xs[:].indirect(offsets[:]))
         for m in (W3, W1):
@@ -153,7 +158,7 @@ def tile_moe_cas_glu_relu_kernel(
             c, lo = divmod(block * BLOCK, CHUNK)
             return hidden[c][:, lo * PACK : (lo + BLOCK) * PACK]
 
-        lin_at = {3: SCALES0}
+        lin_at = {5: LIN5, 6: LIN6}
 
         def linear(block, index):
             if block in lin_at:
@@ -176,10 +181,8 @@ def tile_moe_cas_glu_relu_kernel(
             nc.scalar.activation(out=by_token(act_sb[:]), in_=first_layer(W1, block, index), func=ACT.Relu)
             nc.gpsimd.tensor_tensor(out=hidden_part(block), in0=act_sb[:], in1=lin_sb[block][:], op=ALU.mult)
 
-        codes = [shared("codes%d" % c, CHUNK, U32, at) for c, at in enumerate((CODES0,))]
-        codes.extend([kept("codes%d" % c, CHUNK, U32) for c in range(1, chunks)])
-        scales = [shared("scales%d" % c, CHUNK, U8, at) for c, at in enumerate((SCALES0,))]
-        scales.extend([kept("scales%d" % c, CHUNK, U8) for c in range(1, chunks)])
+        codes = [kept("codes%d" % c, CHUNK, U32) if c != 1 else shared("codes1", CHUNK, U32, CODES1) for c in range(chunks)]
+        scales = [kept("scales%d" % c, CHUNK, U8) if c != 1 else shared("scales1", CHUNK, U8, SCALES1) for c in range(chunks)]
 
         def quantize(c):
             nc.vector.quantize_mx(out=codes[c][:].bitcast(FP8X4), scales=scales[c][:], in_=hidden[c][:])
@@ -211,43 +214,49 @@ def tile_moe_cas_glu_relu_kernel(
         gate_on_vector(0, 5)
         linear(1, 6)
         gate_on_vector(1, 7)
+        linear(2, 2)
+        gate_on_vector(2, 3)
         quantize(0)
         light(0, 2, 4)
-        linear(2, 5)
-        gate_on_vector(2, 7)
-        light(0, 3, 6)
+        linear(3, 6)
+        gate_on_vector(3, 5)
+        quantize(1)
+        light(0, 3, 2)
         down00 = second_layer(0, 0, (0,))
         down10 = second_layer(0, 1, (1,))
         z00 = kept("z0_0", CHUNK, F32)
         bring(down00[:], 0, 0, z00)
-        z10 = shared("z1_0", CHUNK, F32, CODES0)
+        z10 = kept("z1_0", CHUNK, F32)
         nc.scalar.copy(out=z10[:], in_=down10[:])
-        linear(3, 4)
-        gate_on_vector(3, 7)
-        quantize(1)
-        light(1, 2, 0)
-        light(1, 3, 1)
+        light(1, 2, 5)
+        light(1, 3, 0)
         scatter(1, 0, z10[:])
-        linear(4, 4)
-        gate_on_gpsimd(4, 0, kept("act_sb4", BANK, F32))
-        linear(5, 1)
-        down1 = second_layer(1, 2)
+        linear(4, 1)
+        gate_on_gpsimd(4, 5, kept("act_sb4", BANK, F32))
+        down1 = second_layer(1, 7)
         bring(down1[:, :CHUNK], 0, 1, kept("z0_1", CHUNK, F32))
-        gate_on_gpsimd(5, 4, shared("act_sb5", BANK, F32, ACT5))
+        linear(5, 0)
+        gate_on_gpsimd(5, 1, shared("act_sb5", BANK, F32, ACT5))
         quantize(2)
-        linear(6, 0)
-        gate_on_gpsimd(6, 1, kept("act_sb6", BANK, F32))
-        linear(7, 4)
+        linear(6, 5)
+        gate_on_gpsimd(6, 0, kept("act_sb6", BANK, F32))
+        linear(7, 1)
         bring(down1[:, CHUNK:], 1, 1, shared("z1_1", CHUNK, F32, ACT5))
-        gate_on_gpsimd(7, 0, shared("act_sb7", BANK, F32, ACT7))
+        gate_on_gpsimd(7, 5, shared("act_sb7", BANK, F32, ACT7))
         down2 = second_layer(2, 3)
         bring(down2[:, :CHUNK], 0, 2, kept("z0_2", CHUNK, F32))
         quantize(3)
-        bring(down2[:, CHUNK:], 1, 2, shared("z1_2", CHUNK, F32, ACT7))
-        down3 = second_layer(3, 5)
-        last = kept("z_last", 2 * CHUNK, F32)
-        nc.scalar.copy(out=last[:], in_=down3[:])
-        scatter(0, 3, last[:, :CHUNK])
+        last = shared("z_last", 2 * CHUNK, F32, ACT7)
+        nc.scalar.copy(out=last[:, :CHUNK], in_=down2[:, CHUNK:])
+        nc.vector.tensor_tensor(
+            window[1][:].indirect(list_part(2 * CHUNK, FILL)), last[:, :FILL], zeros[:], ALU.add
+        )
+        down03 = second_layer(3, 4, (0,))
+        down13 = second_layer(3, 6, (1,))
+        bring(down03[:], 0, 3, kept("z0_3", CHUNK, F32))
+        nc.scalar.copy(out=last[:, CHUNK:], in_=down13[:])
         nc.sync.dma_start(out=out[0:P, :], in_=window[0][:])
-        scatter(1, 3, last[:, CHUNK:])
+        nc.vector.tensor_copy(
+            window[1][:].indirect(list_part(2 * CHUNK + FILL, 2 * CHUNK - FILL)), last[:, FILL:]
+        )
         nc.sync.dma_start(out=out[P : 2 * P, :], in_=window[1][:])

@@ -25,8 +25,7 @@ CHUNK = 256
 PER_COL = 16
 FILL = 192
 W1, W3 = 0, 1
-RAW3 = 4096
-LIN5 = 8192
+LIN5 = 0
 LIN6 = LIN5 + BANK_BYTES
 CODES1 = LIN6 - 512
 SCALES1 = LIN6 + BANK_BYTES
@@ -69,17 +68,16 @@ def tile_moe_cas_glu_relu_kernel(
         width = 2 * H + N
         staged = keep.tile([16, width], U8, name="staged", align_bytes=64)
         planes = kept("planes", width, U8)
-        raw = [shared("raw%d" % m, 2 * H, U8, at) for m, at in ((W1, RAW3), (W3, 0))]
+        raw = [kept("raw%d" % m, 2 * H, U8) for m in (W1, W3)]
         up = [kept("up%d" % m, 2 * H, U8) for m in (W1, W3)]
 
         def list_part(first, count):
             return offsets[:, first // PER_COL : (first + count) // PER_COL]
 
-        for plane in (xs, w2_plane):
+        for plane in (xs, planes, w2_plane):
             nc.vector.memset(plane[:].bitcast(I32), 0)
         words = x_words[0].rearrange("p t d -> p (t d)").bitcast(I32)
         nc.gpsimd.dma_start(out=xw[:, : T // 2], in_=words[:, : T // 2])
-        nc.gpsimd.memset(planes[:].bitcast(I32), 0)
         nc.gpsimd.dma_start(out=xw[:, T // 2 :], in_=words[:, T // 2 :])
         nc.sync.dma_start(offsets[:], offs)
         lo = 0
@@ -102,13 +100,13 @@ def tile_moe_cas_glu_relu_kernel(
         gs = kept("gs", S, U8)
         nc.vector.tensor_copy(gs[:], xs[:].indirect(offsets[:]))
         for m in (W3, W1):
-            nc.vector.tensor_copy(
+            nc.gpsimd.tensor_copy(
                 out=up[m][:].bitcast(U16).rearrange("p (t m) -> p t m", t=PACK),
                 in_=raw[m][:].bitcast(U16).rearrange("p (m t) -> p t m", t=PACK),
             )
-        gw = shared("gw", S, U32, RAW3 + H - 4 * S)
+        gw = kept("gw", S, U32)
         nc.vector.tensor_copy(gw[:, :CHUNK], xw[:].bitcast(U32).indirect(list_part(0, CHUNK)))
-        ups = shared("ups", 2 * H, U8, RAW3 + H)
+        ups = kept("ups", 2 * H, U8)
         for m in (W3, W1):
             nc.gpsimd.tensor_copy(
                 out=ups[:, m * H : (m + 1) * H].rearrange("p (t m) -> p t m", t=PACK),
@@ -214,36 +212,36 @@ def tile_moe_cas_glu_relu_kernel(
         gate_on_vector(0, 5)
         linear(1, 6)
         gate_on_vector(1, 7)
-        linear(2, 2)
-        gate_on_vector(2, 3)
+        light(0, 2, 2)
+        linear(2, 4)
+        gate_on_vector(2, 5)
         quantize(0)
-        light(0, 2, 4)
         linear(3, 6)
-        gate_on_vector(3, 5)
+        gate_on_vector(3, 7)
         quantize(1)
-        light(0, 3, 2)
+        light(0, 3, 3)
+        light(1, 2, 2)
         down00 = second_layer(0, 0, (0,))
         down10 = second_layer(0, 1, (1,))
         z00 = kept("z0_0", CHUNK, F32)
         bring(down00[:], 0, 0, z00)
         z10 = kept("z1_0", CHUNK, F32)
         nc.scalar.copy(out=z10[:], in_=down10[:])
-        light(1, 2, 5)
-        light(1, 3, 0)
+        light(1, 3, 7)
         scatter(1, 0, z10[:])
-        linear(4, 1)
-        gate_on_gpsimd(4, 5, kept("act_sb4", BANK, F32))
-        down1 = second_layer(1, 7)
+        linear(4, 0)
+        gate_on_gpsimd(4, 1, kept("act_sb4", BANK, F32))
+        down1 = second_layer(1, 3)
         bring(down1[:, :CHUNK], 0, 1, kept("z0_1", CHUNK, F32))
-        linear(5, 0)
-        gate_on_gpsimd(5, 1, shared("act_sb5", BANK, F32, ACT5))
+        linear(5, 7)
+        gate_on_gpsimd(5, 0, shared("act_sb5", BANK, F32, ACT5))
         quantize(2)
-        linear(6, 5)
-        gate_on_gpsimd(6, 0, kept("act_sb6", BANK, F32))
-        linear(7, 1)
+        linear(6, 1)
+        gate_on_gpsimd(6, 7, kept("act_sb6", BANK, F32))
+        linear(7, 0)
         bring(down1[:, CHUNK:], 1, 1, shared("z1_1", CHUNK, F32, ACT5))
-        gate_on_gpsimd(7, 5, shared("act_sb7", BANK, F32, ACT7))
-        down2 = second_layer(2, 3)
+        gate_on_gpsimd(7, 1, shared("act_sb7", BANK, F32, ACT7))
+        down2 = second_layer(2, 4)
         bring(down2[:, :CHUNK], 0, 2, kept("z0_2", CHUNK, F32))
         quantize(3)
         last = shared("z_last", 2 * CHUNK, F32, ACT7)
@@ -251,7 +249,7 @@ def tile_moe_cas_glu_relu_kernel(
         nc.vector.tensor_tensor(
             window[1][:].indirect(list_part(2 * CHUNK, FILL)), last[:, :FILL], zeros[:], ALU.add
         )
-        down03 = second_layer(3, 4, (0,))
+        down03 = second_layer(3, 5, (0,))
         down13 = second_layer(3, 6, (1,))
         bring(down03[:], 0, 3, kept("z0_3", CHUNK, F32))
         nc.scalar.copy(out=last[:, CHUNK:], in_=down13[:])

@@ -25,7 +25,8 @@ CHUNK = 256
 PER_COL = 16
 FILL = 192
 W1, W3 = 0, 1
-LIN5 = 0
+RAW3 = 4096
+LIN5 = 8192
 LIN6 = LIN5 + BANK_BYTES
 CODES1 = LIN6 - 512
 SCALES1 = LIN6 + BANK_BYTES
@@ -68,7 +69,7 @@ def tile_moe_cas_glu_relu_kernel(
         width = 2 * H + N
         staged = keep.tile([16, width], U8, name="staged", align_bytes=64)
         planes = kept("planes", width, U8)
-        raw = [kept("raw%d" % m, 2 * H, U8) for m in (W1, W3)]
+        raw = [shared("raw%d" % m, 2 * H, U8, at) for m, at in ((W1, RAW3), (W3, 0))]
         up = [kept("up%d" % m, 2 * H, U8) for m in (W1, W3)]
 
         def list_part(first, count):
@@ -100,13 +101,13 @@ def tile_moe_cas_glu_relu_kernel(
         gs = kept("gs", S, U8)
         nc.vector.tensor_copy(gs[:], xs[:].indirect(offsets[:]))
         for m in (W3, W1):
-            nc.gpsimd.tensor_copy(
+            nc.vector.tensor_copy(
                 out=up[m][:].bitcast(U16).rearrange("p (t m) -> p t m", t=PACK),
                 in_=raw[m][:].bitcast(U16).rearrange("p (m t) -> p t m", t=PACK),
             )
-        gw = kept("gw", S, U32)
+        gw = shared("gw", S, U32, RAW3 + H - 4 * S)
         nc.vector.tensor_copy(gw[:, :CHUNK], xw[:].bitcast(U32).indirect(list_part(0, CHUNK)))
-        ups = kept("ups", 2 * H, U8)
+        ups = shared("ups", 2 * H, U8, RAW3 + H)
         for m in (W3, W1):
             nc.gpsimd.tensor_copy(
                 out=ups[:, m * H : (m + 1) * H].rearrange("p (t m) -> p t m", t=PACK),

@@ -75,10 +75,13 @@ def tile_moe_cas_glu_relu_kernel(
         def list_part(first, count):
             return offsets[:, first // PER_COL : (first + count) // PER_COL]
 
-        for plane in (xs, planes, w2_plane):
-            nc.vector.memset(plane[:].bitcast(I32), 0)
+        nc.vector.memset(xs[:].bitcast(I32), 0)
         words = x_words[0].rearrange("p t d -> p (t d)").bitcast(I32)
         nc.gpsimd.dma_start(out=xw[:, : T // 2], in_=words[:, : T // 2])
+        zeros = kept("zeros", FILL, F32)
+        for plane in (planes[:, :H], planes[:, H : 2 * H], planes[:, 2 * H :], w2_plane[:]):
+            nc.gpsimd.memset(plane.bitcast(I32), 0)
+        nc.gpsimd.memset(zeros[:], 0.0)
         nc.gpsimd.dma_start(out=xw[:, T // 2 :], in_=words[:, T // 2 :])
         nc.sync.dma_start(offsets[:], offs)
         lo = 0
@@ -96,8 +99,6 @@ def tile_moe_cas_glu_relu_kernel(
         load_scale_rows([nc.sync] * 4, w2_plane, w2_scales[0])
         w_plane = planes[:, 2 * H :]
 
-        zeros = kept("zeros", FILL, F32)
-        nc.vector.memset(zeros[:], 0.0)
         gs = kept("gs", S, U8)
         nc.vector.tensor_copy(gs[:], xs[:].indirect(offsets[:]))
         for m in (W3, W1):

@@ -23,16 +23,10 @@ BANK_BYTES = 2048
 BLOCK = 128
 CHUNK = 256
 PER_COL = 16
-FILL = 192
 W1, W3 = 0, 1
-RAW3 = 4096
-LIN5 = 8192
-LIN6 = LIN5 + BANK_BYTES
-CODES1 = LIN6 - 512
-SCALES1 = LIN6 + BANK_BYTES
-HIDDEN = SCALES1 + BANK_BYTES
-ACT5 = SCALES1
-ACT7 = HIDDEN + BANK_BYTES
+RAW1 = 4096
+LINEAR_BANKS = (5, 0, 1, 3, 4, 5, 0, 1)
+GATE_BANKS = (6, 7, 2, 6, 7, 2, 6, 7)
 
 
 def load_scale_rows(queues, plane, rows):
@@ -69,7 +63,7 @@ def tile_moe_cas_glu_relu_kernel(
         width = 2 * H + N
         staged = keep.tile([16, width], U8, name="staged", align_bytes=64)
         planes = kept("planes", width, U8)
-        raw = [shared("raw%d" % m, 2 * H, U8, at) for m, at in ((W1, RAW3), (W3, 0))]
+        raw = [shared("raw%d" % m, 2 * H, U8, at) for m, at in ((W1, RAW1), (W3, 0))]
         up = [kept("up%d" % m, 2 * H, U8) for m in (W1, W3)]
 
         def list_part(first, count):
@@ -78,10 +72,8 @@ def tile_moe_cas_glu_relu_kernel(
         nc.vector.memset(xs[:].bitcast(I32), 0)
         words = x_words[0].rearrange("p t d -> p (t d)").bitcast(I32)
         nc.gpsimd.dma_start(out=xw[:, : T // 2], in_=words[:, : T // 2])
-        zeros = kept("zeros", FILL, F32)
         for plane in (planes[:, :H], planes[:, H : 2 * H], planes[:, 2 * H :], w2_plane[:]):
             nc.gpsimd.memset(plane.bitcast(I32), 0)
-        nc.gpsimd.memset(zeros[:], 0.0)
         nc.gpsimd.dma_start(out=xw[:, T // 2 :], in_=words[:, T // 2 :])
         nc.sync.dma_start(offsets[:], offs)
         lo = 0
@@ -106,9 +98,9 @@ def tile_moe_cas_glu_relu_kernel(
                 out=up[m][:].bitcast(U16).rearrange("p (t m) -> p t m", t=PACK),
                 in_=raw[m][:].bitcast(U16).rearrange("p (m t) -> p t m", t=PACK),
             )
-        gw = shared("gw", S, U32, RAW3 + H - 4 * S)
+        gw = shared("gw", S, U32, RAW1 + H - 4 * S)
         nc.vector.tensor_copy(gw[:, :CHUNK], xw[:].bitcast(U32).indirect(list_part(0, CHUNK)))
-        ups = shared("ups", 2 * H, U8, RAW3 + H)
+        ups = shared("ups", 2 * H, U8, RAW1 + H)
         for m in (W3, W1):
             nc.gpsimd.tensor_copy(
                 out=ups[:, m * H : (m + 1) * H].rearrange("p (t m) -> p t m", t=PACK),
@@ -147,51 +139,35 @@ def tile_moe_cas_glu_relu_kernel(
                 )
             return acc[:].rearrange("p t n -> p n t")
 
-        hidden = [kept("hidden%d" % c, CHUNK * PACK, BF16) for c in range(1)]
-        hidden.extend([shared("hidden%d" % c, CHUNK * PACK, BF16, HIDDEN) for c in range(1, chunks)])
-        lin_sb = {}
+        hidden = [kept("hidden%d" % c, CHUNK * PACK, BF16) for c in range(chunks)]
+        lin = [kept("lin%d" % block, BANK, F32) for block in range(S // BLOCK)]
+        codes = [kept("codes%d" % c, CHUNK, U32) for c in range(chunks)]
+        scales = [kept("scales%d" % c, CHUNK, U8) for c in range(chunks)]
+        z = [kept("z%d" % c, 2 * CHUNK, F32) for c in range(chunks)]
 
         def by_token(ap):
             return ap.rearrange("p (n t) -> p n t", t=PACK)
 
-        def hidden_part(block):
+        def gated(block):
             c, lo = divmod(block * BLOCK, CHUNK)
-            return hidden[c][:, lo * PACK : (lo + BLOCK) * PACK]
-
-        lin_at = {5: LIN5, 6: LIN6}
-
-        def linear(block, index):
-            if block in lin_at:
-                lin_sb[block] = shared("lin_sb%d" % block, BANK, F32, lin_at[block])
-            else:
-                lin_sb[block] = kept("lin_sb%d" % block, BANK, F32)
-            nc.scalar.copy(out=by_token(lin_sb[block][:]), in_=first_layer(W3, block, index))
-
-        def gate_on_vector(block, index):
+            nc.scalar.copy(out=by_token(lin[block][:]), in_=first_layer(W3, block, LINEAR_BANKS[block]))
             nc.vector.scalar_tensor_tensor(
-                out=by_token(hidden_part(block)),
-                in0=first_layer(W1, block, index),
+                out=by_token(hidden[c][:, lo * PACK : (lo + BLOCK) * PACK]),
+                in0=first_layer(W1, block, GATE_BANKS[block]),
                 scalar=0.0,
-                in1=by_token(lin_sb[block][:]),
+                in1=by_token(lin[block][:]),
                 op0=ALU.max,
                 op1=ALU.mult,
             )
 
-        def gate_on_gpsimd(block, index, act_sb):
-            nc.scalar.activation(out=by_token(act_sb[:]), in_=first_layer(W1, block, index), func=ACT.Relu)
-            nc.gpsimd.tensor_tensor(out=hidden_part(block), in0=act_sb[:], in1=lin_sb[block][:], op=ALU.mult)
-
-        codes = [kept("codes%d" % c, CHUNK, U32) if c != 1 else shared("codes1", CHUNK, U32, CODES1) for c in range(chunks)]
-        scales = [kept("scales%d" % c, CHUNK, U8) if c != 1 else shared("scales1", CHUNK, U8, SCALES1) for c in range(chunks)]
-
         def quantize(c):
             nc.vector.quantize_mx(out=codes[c][:].bitcast(FP8X4), scales=scales[c][:], in_=hidden[c][:])
 
-        def second_layer(c, index, blocks=(0, 1)):
-            acc = bank("down%d_%d" % (c, blocks[0]), [P, len(blocks) * CHUNK], index)
-            for at, b in enumerate(blocks):
+        def second_layer(c, index):
+            acc = bank("down%d" % c, [P, 2 * CHUNK], index)
+            for b in range(2):
                 nc.tensor.matmul_mx(
-                    out=acc[:, at * CHUNK : (at + 1) * CHUNK],
+                    out=acc[:, b * CHUNK : (b + 1) * CHUNK],
                     lhsT=w2w[:, 2 * P * b : 2 * P * (b + 1)].bitcast(FP4X4),
                     lhsT_scale=w2_plane[:, P * b : P * (b + 1)],
                     rhs=codes[c][:].bitcast(FP8X4),
@@ -199,64 +175,36 @@ def tile_moe_cas_glu_relu_kernel(
                     start=True,
                     stop=True,
                 )
-            return acc
+            nc.scalar.copy(out=z[c][:], in_=acc[:])
 
-        def scatter(b, c, z):
-            nc.vector.tensor_copy(window[b][:].indirect(list_part(c * CHUNK, z.shape[1])), z)
+        def scatter_on_vector(b, c):
+            target = window[b][:].indirect(list_part(c * CHUNK, CHUNK))
+            nc.vector.tensor_copy(target, z[c][:, b * CHUNK : (b + 1) * CHUNK])
 
-        def bring(acc, b, c, z):
-            nc.scalar.copy(out=z[:], in_=acc)
-            scatter(b, c, z[:])
+        def scatter_on_scalar(b, c):
+            target = window[b][:].indirect(list_part(c * CHUNK, CHUNK))
+            nc.scalar.activation(out=target, in_=z[c][:, b * CHUNK : (b + 1) * CHUNK], func=ACT.Copy)
 
-        for index, (b, j) in enumerate(((0, 0), (0, 1), (1, 0), (1, 1))):
+        for index, (b, j) in enumerate(((0, 0), (0, 1), (1, 0), (1, 1), (0, 2))):
             light(b, j, index)
-        linear(0, 4)
-        gate_on_vector(0, 5)
-        linear(1, 6)
-        gate_on_vector(1, 7)
-        light(0, 2, 2)
-        linear(2, 4)
-        gate_on_vector(2, 5)
-        quantize(0)
-        linear(3, 6)
-        gate_on_vector(3, 7)
-        quantize(1)
+        for block in range(S // BLOCK):
+            gated(block)
+            if block in (2, 4, 6):
+                quantize(block // 2 - 1)
         light(0, 3, 3)
-        light(1, 2, 2)
-        down00 = second_layer(0, 0, (0,))
-        down10 = second_layer(0, 1, (1,))
-        z00 = kept("z0_0", CHUNK, F32)
-        bring(down00[:], 0, 0, z00)
-        z10 = kept("z1_0", CHUNK, F32)
-        nc.scalar.copy(out=z10[:], in_=down10[:])
-        light(1, 3, 7)
-        scatter(1, 0, z10[:])
-        linear(4, 0)
-        gate_on_gpsimd(4, 1, kept("act_sb4", BANK, F32))
-        down1 = second_layer(1, 3)
-        bring(down1[:, :CHUNK], 0, 1, kept("z0_1", CHUNK, F32))
-        linear(5, 7)
-        gate_on_gpsimd(5, 0, shared("act_sb5", BANK, F32, ACT5))
-        quantize(2)
-        linear(6, 1)
-        gate_on_gpsimd(6, 7, kept("act_sb6", BANK, F32))
-        linear(7, 0)
-        bring(down1[:, CHUNK:], 1, 1, shared("z1_1", CHUNK, F32, ACT5))
-        gate_on_gpsimd(7, 1, shared("act_sb7", BANK, F32, ACT7))
-        down2 = second_layer(2, 4)
-        bring(down2[:, :CHUNK], 0, 2, kept("z0_2", CHUNK, F32))
+        second_layer(0, 4)
+        scatter_on_vector(0, 0)
         quantize(3)
-        last = shared("z_last", 2 * CHUNK, F32, ACT7)
-        nc.scalar.copy(out=last[:, :CHUNK], in_=down2[:, CHUNK:])
-        nc.vector.tensor_tensor(
-            window[1][:].indirect(list_part(2 * CHUNK, FILL)), last[:, :FILL], zeros[:], ALU.add
-        )
-        down03 = second_layer(3, 5, (0,))
-        down13 = second_layer(3, 6, (1,))
-        bring(down03[:], 0, 3, kept("z0_3", CHUNK, F32))
-        nc.scalar.copy(out=last[:, CHUNK:], in_=down13[:])
+        light(1, 2, 5)
+        light(1, 3, 0)
+        second_layer(1, 1)
+        scatter_on_vector(0, 1)
+        second_layer(2, 3)
+        scatter_on_vector(0, 2)
+        scatter_on_scalar(1, 0)
+        second_layer(3, 4)
+        scatter_on_vector(0, 3)
         nc.sync.dma_start(out=out[0:P, :], in_=window[0][:])
-        nc.vector.tensor_copy(
-            window[1][:].indirect(list_part(2 * CHUNK + FILL, 2 * CHUNK - FILL)), last[:, FILL:]
-        )
+        for c in range(1, chunks):
+            scatter_on_scalar(1, c)
         nc.sync.dma_start(out=out[P : 2 * P, :], in_=window[1][:])

@@ -22,11 +22,12 @@ BANK = 512
 BANK_BYTES = 2048
 BLOCK = 128
 CHUNK = 256
+HALF = 512
+WIDE = 384
 PER_COL = 16
 W1, W3 = 0, 1
-RAW1 = 4096
 LINEAR_BANKS = (5, 0, 1, 3, 4, 5, 0, 1)
-GATE_BANKS = (6, 7, 2, 6, 7, 2, 6, 7)
+GATE_BANKS = (6, 7, 2, 6, 7, 2, 6, 5)
 
 
 def load_scale_rows(queues, plane, rows):
@@ -39,17 +40,12 @@ def tile_moe_cas_glu_relu_kernel(
     tc, x_words, x_scales, w_words, w_scales, w1_words, w1_scales, w3_words, w3_scales, w2_words, w2_scales, offs, out
 ):
     nc = tc.nc
-    chunks = S // CHUNK
     with ExitStack() as ctx:
         keep = ctx.enter_context(tc.tile_pool(name="keep", bufs=1))
-        reuse = ctx.enter_context(tc.tile_pool(name="reuse", bufs=1))
         psum = ctx.enter_context(tc.psum_pool(name="psum", bufs=1))
 
         def kept(name, width, dtype):
             return keep.tile([P, width], dtype, name=name, align_bytes=64)
-
-        def shared(name, width, dtype, offset):
-            return reuse.tile([P, width], dtype, name=name, offset=offset, align_bytes=64)
 
         def bank(name, shape, index):
             return psum.tile(shape, F32, name=name, offset=index * BANK_BYTES)
@@ -63,7 +59,7 @@ def tile_moe_cas_glu_relu_kernel(
         width = 2 * H + N
         staged = keep.tile([16, width], U8, name="staged", align_bytes=64)
         planes = kept("planes", width, U8)
-        raw = [shared("raw%d" % m, 2 * H, U8, at) for m, at in ((W1, RAW1), (W3, 0))]
+        raw = [kept("raw%d" % m, 2 * H, U8) for m in (W1, W3)]
         up = [kept("up%d" % m, 2 * H, U8) for m in (W1, W3)]
 
         def list_part(first, count):
@@ -93,20 +89,19 @@ def tile_moe_cas_glu_relu_kernel(
 
         gs = kept("gs", S, U8)
         nc.vector.tensor_copy(gs[:], xs[:].indirect(offsets[:]))
+        ups = kept("ups", 2 * H, U8)
         for m in (W3, W1):
-            nc.vector.tensor_copy(
+            nc.gpsimd.tensor_copy(
                 out=up[m][:].bitcast(U16).rearrange("p (t m) -> p t m", t=PACK),
                 in_=raw[m][:].bitcast(U16).rearrange("p (m t) -> p t m", t=PACK),
             )
-        gw = shared("gw", S, U32, RAW1 + H - 4 * S)
-        nc.vector.tensor_copy(gw[:, :CHUNK], xw[:].bitcast(U32).indirect(list_part(0, CHUNK)))
-        ups = shared("ups", 2 * H, U8, RAW1 + H)
-        for m in (W3, W1):
             nc.gpsimd.tensor_copy(
                 out=ups[:, m * H : (m + 1) * H].rearrange("p (t m) -> p t m", t=PACK),
                 in_=planes[:, m * H : (m + 1) * H].rearrange("p (m t) -> p t m", t=PACK),
             )
-        nc.vector.tensor_copy(gw[:, CHUNK:], xw[:].bitcast(U32).indirect(list_part(CHUNK, S - CHUNK)))
+        gw = kept("gw", S, U32)
+        for first, count in ((0, CHUNK), (CHUNK, CHUNK), (HALF, HALF)):
+            nc.vector.tensor_copy(gw[:, first : first + count], xw[:].bitcast(U32).indirect(list_part(first, count)))
 
         window = [kept("window0", T, F32), kept("window1", T, F32)]
 
@@ -139,20 +134,22 @@ def tile_moe_cas_glu_relu_kernel(
                 )
             return acc[:].rearrange("p t n -> p n t")
 
-        hidden = [kept("hidden%d" % c, CHUNK * PACK, BF16) for c in range(chunks)]
+        parts = ((0, HALF), (HALF, CHUNK), (HALF + CHUNK, CHUNK))
+        hidden = [kept("hidden%d" % i, count * PACK, BF16) for i, (first, count) in enumerate(parts)]
+        codes = [kept("codes%d" % i, count, U32) for i, (first, count) in enumerate(parts)]
+        scales = [kept("scales%d" % i, count, U8) for i, (first, count) in enumerate(parts)]
         lin = [kept("lin%d" % block, BANK, F32) for block in range(S // BLOCK)]
-        codes = [kept("codes%d" % c, CHUNK, U32) for c in range(chunks)]
-        scales = [kept("scales%d" % c, CHUNK, U8) for c in range(chunks)]
-        z = [kept("z%d" % c, 2 * CHUNK, F32) for c in range(chunks)]
+        z = kept("z", 2 * S, F32)
 
         def by_token(ap):
             return ap.rearrange("p (n t) -> p n t", t=PACK)
 
         def gated(block):
-            c, lo = divmod(block * BLOCK, CHUNK)
+            part = max(i for i, (first, count) in enumerate(parts) if first <= block * BLOCK)
+            lo = block * BLOCK - parts[part][0]
             nc.scalar.copy(out=by_token(lin[block][:]), in_=first_layer(W3, block, LINEAR_BANKS[block]))
             nc.vector.scalar_tensor_tensor(
-                out=by_token(hidden[c][:, lo * PACK : (lo + BLOCK) * PACK]),
+                out=by_token(hidden[part][:, lo * PACK : (lo + BLOCK) * PACK]),
                 in0=first_layer(W1, block, GATE_BANKS[block]),
                 scalar=0.0,
                 in1=by_token(lin[block][:]),
@@ -160,51 +157,56 @@ def tile_moe_cas_glu_relu_kernel(
                 op1=ALU.mult,
             )
 
-        def quantize(c):
-            nc.vector.quantize_mx(out=codes[c][:].bitcast(FP8X4), scales=scales[c][:], in_=hidden[c][:])
+        def quantize(part):
+            nc.vector.quantize_mx(out=codes[part][:].bitcast(FP8X4), scales=scales[part][:], in_=hidden[part][:])
 
-        def second_layer(c, index):
-            acc = bank("down%d" % c, [P, 2 * CHUNK], index)
-            for b in range(2):
+        def second_layer(part, row_blocks, index):
+            first, count = parts[part]
+            acc = bank("down%d_%d" % (part, row_blocks[0]), [P, len(row_blocks), count], index)
+            for at, b in enumerate(row_blocks):
                 nc.tensor.matmul_mx(
-                    out=acc[:, b * CHUNK : (b + 1) * CHUNK],
+                    out=acc[:, at, :],
                     lhsT=w2w[:, 2 * P * b : 2 * P * (b + 1)].bitcast(FP4X4),
                     lhsT_scale=w2_plane[:, P * b : P * (b + 1)],
-                    rhs=codes[c][:].bitcast(FP8X4),
-                    rhs_scale=scales[c][:],
+                    rhs=codes[part][:].bitcast(FP8X4),
+                    rhs_scale=scales[part][:],
                     start=True,
                     stop=True,
                 )
-            nc.scalar.copy(out=z[c][:], in_=acc[:])
+            rows = z[:].rearrange("p (b s) -> p b s", b=2)[:, row_blocks[0] : row_blocks[-1] + 1, first : first + count]
+            nc.scalar.copy(out=rows, in_=acc[:])
 
-        def scatter_on_vector(b, c):
-            target = window[b][:].indirect(list_part(c * CHUNK, CHUNK))
-            nc.vector.tensor_copy(target, z[c][:, b * CHUNK : (b + 1) * CHUNK])
+        def scatter_on_vector(b, first, count):
+            nc.vector.tensor_copy(
+                window[b][:].indirect(list_part(first, count)), z[:, b * S + first : b * S + first + count]
+            )
 
-        def scatter_on_scalar(b, c):
-            target = window[b][:].indirect(list_part(c * CHUNK, CHUNK))
-            nc.scalar.activation(out=target, in_=z[c][:, b * CHUNK : (b + 1) * CHUNK], func=ACT.Copy)
+        def scatter_on_scalar(b, first, count):
+            nc.scalar.activation(
+                out=window[b][:].indirect(list_part(first, count)),
+                in_=z[:, b * S + first : b * S + first + count],
+                func=ACT.Copy,
+            )
 
         for index, (b, j) in enumerate(((0, 0), (0, 1), (1, 0), (1, 1), (0, 2))):
             light(b, j, index)
         for block in range(S // BLOCK):
             gated(block)
-            if block in (2, 4, 6):
-                quantize(block // 2 - 1)
+            if block in (4, 6):
+                quantize(block // 2 - 2)
         light(0, 3, 3)
-        second_layer(0, 4)
-        scatter_on_vector(0, 0)
-        quantize(3)
-        light(1, 2, 5)
-        light(1, 3, 0)
-        second_layer(1, 1)
-        scatter_on_vector(0, 1)
-        second_layer(2, 3)
-        scatter_on_vector(0, 2)
-        scatter_on_scalar(1, 0)
-        second_layer(3, 4)
-        scatter_on_vector(0, 3)
+        second_layer(0, (0,), 4)
+        scatter_on_vector(0, 0, CHUNK)
+        quantize(2)
+        light(1, 2, 7)
+        light(1, 3, 2)
+        second_layer(0, (1,), 1)
+        second_layer(1, (0, 1), 0)
+        scatter_on_vector(0, CHUNK, HALF)
+        scatter_on_scalar(1, 0, WIDE)
+        second_layer(2, (0, 1), 0)
+        scatter_on_vector(0, S - CHUNK, CHUNK)
         nc.sync.dma_start(out=out[0:P, :], in_=window[0][:])
-        for c in range(1, chunks):
-            scatter_on_scalar(1, c)
+        scatter_on_scalar(1, S - WIDE, WIDE)
+        scatter_on_scalar(1, WIDE, S - 2 * WIDE)
         nc.sync.dma_start(out=out[P : 2 * P, :], in_=window[1][:])

@@ -71,17 +71,15 @@ def tile_moe_cas_glu_relu_kernel(
         for plane in (planes[:, :H], planes[:, H : 2 * H], planes[:, 2 * H :], w2_plane[:]):
             nc.gpsimd.memset(plane.bitcast(I32), 0)
         nc.gpsimd.dma_start(out=xw[:, T // 2 :], in_=words[:, T // 2 :])
+        nc.sync.dma_start(out=staged[:, 2 * H :].bitcast(I32), in_=w_scales[0].bitcast(I32))
+        nc.scalar.dma_start(out=staged[:, H : 2 * H].bitcast(I32), in_=w3_scales[0].bitcast(I32))
         nc.sync.dma_start(offsets[:], offs)
-        lo = 0
-        for queue, source in ((nc.scalar, w1_scales), (nc.sync, w3_scales), (nc.scalar, w_scales)):
-            hi = lo + source.shape[2]
-            queue.dma_start(out=staged[:, lo:hi].bitcast(I32), in_=source[0].bitcast(I32))
-            lo = hi
-        load_scale_rows([nc.sync, nc.scalar] * 2, xs, x_scales[0])
-        nc.sync.dma_start(out=raw[W3][:].bitcast(I32), in_=w3_words[0].bitcast(I32))
-        nc.scalar.dma_start(out=ww[:].bitcast(I32), in_=w_words[0].bitcast(I32))
-        for r, queue in enumerate([nc.sync, nc.scalar] * 2):
+        nc.scalar.dma_start(out=staged[:, :H].bitcast(I32), in_=w1_scales[0].bitcast(I32))
+        load_scale_rows([nc.sync, nc.scalar, nc.sync, nc.sync], xs, x_scales[0])
+        nc.sync.dma_start(out=ww[:].bitcast(I32), in_=w_words[0].bitcast(I32))
+        for r, queue in enumerate([nc.scalar, nc.sync] * 2):
             queue.dma_start(out=planes[r:P:32, :].bitcast(I32), in_=staged[r:16:4, :].bitcast(I32))
+        nc.sync.dma_start(out=raw[W3][:].bitcast(I32), in_=w3_words[0].bitcast(I32))
         nc.sync.dma_start(out=raw[W1][:].bitcast(I32), in_=w1_words[0].bitcast(I32))
         nc.sync.dma_start(out=w2w[:].bitcast(I32), in_=w2_words[0].bitcast(I32))
         load_scale_rows([nc.sync] * 4, w2_plane, w2_scales[0])
@@ -105,7 +103,7 @@ def tile_moe_cas_glu_relu_kernel(
 
         window = [kept("window0", T, F32), kept("window1", T, F32)]
 
-        def light(b, j, index):
+        def light(b, j, index, evacuate):
             cols = slice(j * BANK, (j + 1) * BANK)
             acc = bank("light%d_%d" % (b, j), [P, BANK], index)
             nc.tensor.matmul_mx(
@@ -117,7 +115,7 @@ def tile_moe_cas_glu_relu_kernel(
                 start=True,
                 stop=True,
             )
-            nc.scalar.copy(out=window[b][:, cols], in_=acc[:])
+            evacuate(out=window[b][:, cols], in_=acc[:])
 
         def first_layer(matrix, block, index):
             acc = bank("pre%d_%d" % (matrix, block), [P, PACK, BLOCK], index)
@@ -189,23 +187,22 @@ def tile_moe_cas_glu_relu_kernel(
             )
 
         for index, (b, j) in enumerate(((0, 0), (0, 1), (1, 0), (1, 1), (0, 2))):
-            light(b, j, index)
+            light(b, j, index, nc.scalar.copy)
         for block in range(S // BLOCK):
             gated(block)
             if block in (4, 6):
                 quantize(block // 2 - 2)
-        light(0, 3, 3)
+        light(0, 3, 3, nc.scalar.copy)
         second_layer(0, (0,), 4)
-        scatter_on_vector(0, 0, CHUNK)
+        light(1, 3, 2, nc.vector.tensor_copy)
         quantize(2)
-        light(1, 2, 7)
-        light(1, 3, 2)
+        scatter_on_vector(0, 0, HALF)
+        light(1, 2, 7, nc.scalar.copy)
         second_layer(0, (1,), 1)
         second_layer(1, (0, 1), 0)
-        scatter_on_vector(0, CHUNK, HALF)
+        second_layer(2, (0, 1), 3)
         scatter_on_scalar(1, 0, WIDE)
-        second_layer(2, (0, 1), 0)
-        scatter_on_vector(0, S - CHUNK, CHUNK)
+        scatter_on_vector(0, HALF, HALF)
         nc.sync.dma_start(out=out[0:P, :], in_=window[0][:])
         scatter_on_scalar(1, S - WIDE, WIDE)
         scatter_on_scalar(1, WIDE, S - 2 * WIDE)

@@ -26,8 +26,8 @@ HALF = 512
 WIDE = 384
 PER_COL = 16
 W1, W3 = 0, 1
-LINEAR_BANKS = (5, 0, 1, 3, 4, 5, 0, 1)
-GATE_BANKS = (6, 7, 2, 6, 7, 2, 6, 5)
+LINEAR_BANKS = (4, 5, 0, 1, 4, 5, 0, 1)
+GATE_BANKS = (6, 7, 2, 3, 6, 7, 2, 3)
 
 
 def load_scale_rows(queues, plane, rows):
@@ -42,6 +42,7 @@ def tile_moe_cas_glu_relu_kernel(
     nc = tc.nc
     with ExitStack() as ctx:
         keep = ctx.enter_context(tc.tile_pool(name="keep", bufs=1))
+        reuse = ctx.enter_context(tc.tile_pool(name="reuse", bufs=1))
         psum = ctx.enter_context(tc.psum_pool(name="psum", bufs=1))
 
         def kept(name, width, dtype):
@@ -59,7 +60,7 @@ def tile_moe_cas_glu_relu_kernel(
         width = 2 * H + N
         staged = keep.tile([16, width], U8, name="staged", align_bytes=64)
         planes = kept("planes", width, U8)
-        raw = [kept("raw%d" % m, 2 * H, U8) for m in (W1, W3)]
+        raw = [reuse.tile([P, 2 * H], U8, name="raw%d" % m, offset=m * 2 * H, align_bytes=64) for m in (W1, W3)]
         up = [kept("up%d" % m, 2 * H, U8) for m in (W1, W3)]
 
         def list_part(first, count):
@@ -71,16 +72,18 @@ def tile_moe_cas_glu_relu_kernel(
         for plane in (planes[:, :H], planes[:, H : 2 * H], planes[:, 2 * H :], w2_plane[:]):
             nc.gpsimd.memset(plane.bitcast(I32), 0)
         nc.gpsimd.dma_start(out=xw[:, T // 2 :], in_=words[:, T // 2 :])
-        nc.sync.dma_start(out=staged[:, 2 * H :].bitcast(I32), in_=w_scales[0].bitcast(I32))
-        nc.scalar.dma_start(out=staged[:, H : 2 * H].bitcast(I32), in_=w3_scales[0].bitcast(I32))
         nc.sync.dma_start(offsets[:], offs)
-        nc.scalar.dma_start(out=staged[:, :H].bitcast(I32), in_=w1_scales[0].bitcast(I32))
-        load_scale_rows([nc.sync, nc.scalar, nc.sync, nc.sync], xs, x_scales[0])
+        lo = 0
+        for queue, source in ((nc.scalar, w1_scales), (nc.sync, w3_scales), (nc.scalar, w_scales)):
+            hi = lo + source.shape[2]
+            queue.dma_start(out=staged[:, lo:hi].bitcast(I32), in_=source[0].bitcast(I32))
+            lo = hi
+        load_scale_rows([nc.sync, nc.scalar] * 2, xs, x_scales[0])
+        nc.sync.dma_start(out=raw[W3][:].bitcast(I32), in_=w3_words[0].bitcast(I32))
+        nc.scalar.dma_start(out=raw[W1][:].bitcast(I32), in_=w1_words[0].bitcast(I32))
         nc.sync.dma_start(out=ww[:].bitcast(I32), in_=w_words[0].bitcast(I32))
         for r, queue in enumerate([nc.scalar, nc.sync] * 2):
             queue.dma_start(out=planes[r:P:32, :].bitcast(I32), in_=staged[r:16:4, :].bitcast(I32))
-        nc.sync.dma_start(out=raw[W3][:].bitcast(I32), in_=w3_words[0].bitcast(I32))
-        nc.sync.dma_start(out=raw[W1][:].bitcast(I32), in_=w1_words[0].bitcast(I32))
         nc.sync.dma_start(out=w2w[:].bitcast(I32), in_=w2_words[0].bitcast(I32))
         load_scale_rows([nc.sync] * 4, w2_plane, w2_scales[0])
         w_plane = planes[:, 2 * H :]
@@ -89,15 +92,16 @@ def tile_moe_cas_glu_relu_kernel(
         nc.vector.tensor_copy(gs[:], xs[:].indirect(offsets[:]))
         ups = kept("ups", 2 * H, U8)
         for m in (W3, W1):
-            nc.gpsimd.tensor_copy(
+            nc.vector.tensor_copy(
                 out=up[m][:].bitcast(U16).rearrange("p (t m) -> p t m", t=PACK),
                 in_=raw[m][:].bitcast(U16).rearrange("p (m t) -> p t m", t=PACK),
             )
+        for m in (W3, W1):
             nc.gpsimd.tensor_copy(
                 out=ups[:, m * H : (m + 1) * H].rearrange("p (t m) -> p t m", t=PACK),
                 in_=planes[:, m * H : (m + 1) * H].rearrange("p (m t) -> p t m", t=PACK),
             )
-        gw = kept("gw", S, U32)
+        gw = reuse.tile([P, S], U32, name="gw", offset=0, align_bytes=64)
         for first, count in ((0, CHUNK), (CHUNK, CHUNK), (HALF, HALF)):
             nc.vector.tensor_copy(gw[:, first : first + count], xw[:].bitcast(U32).indirect(list_part(first, count)))
 
@@ -186,21 +190,22 @@ def tile_moe_cas_glu_relu_kernel(
                 func=ACT.Copy,
             )
 
-        for index, (b, j) in enumerate(((0, 0), (0, 1), (1, 0), (1, 1), (0, 2))):
+        for index, (b, j) in enumerate(((0, 0), (0, 1), (1, 0), (1, 1))):
             light(b, j, index, nc.scalar.copy)
         for block in range(S // BLOCK):
             gated(block)
             if block in (4, 6):
                 quantize(block // 2 - 2)
-        light(0, 3, 3, nc.scalar.copy)
-        second_layer(0, (0,), 4)
-        light(1, 3, 2, nc.vector.tensor_copy)
+        light(0, 2, 4, nc.scalar.copy)
+        light(0, 3, 5, nc.scalar.copy)
+        second_layer(0, (0,), 0)
+        light(1, 3, 6, nc.vector.tensor_copy)
         quantize(2)
         scatter_on_vector(0, 0, HALF)
         light(1, 2, 7, nc.scalar.copy)
         second_layer(0, (1,), 1)
-        second_layer(1, (0, 1), 0)
-        second_layer(2, (0, 1), 3)
+        second_layer(1, (0, 1), 4)
+        second_layer(2, (0, 1), 5)
         scatter_on_scalar(1, 0, WIDE)
         scatter_on_vector(0, HALF, HALF)
         nc.sync.dma_start(out=out[0:P, :], in_=window[0][:])

@@ -26,8 +26,8 @@ HALF = 512
 WIDE = 384
 PER_COL = 16
 W1, W3 = 0, 1
-LINEAR_BANKS = (4, 5, 0, 1, 4, 5, 0, 1)
-GATE_BANKS = (6, 7, 2, 3, 6, 7, 2, 3)
+LINEAR_BANKS = (3, 4, 0, 1, 3, 4, 0, 1)
+GATE_BANKS = (5, 6, 2, 7, 5, 6, 2, 7)
 
 
 def load_scale_rows(queues, plane, rows):
@@ -190,22 +190,23 @@ def tile_moe_cas_glu_relu_kernel(
                 func=ACT.Copy,
             )
 
-        for index, (b, j) in enumerate(((0, 0), (0, 1), (1, 0), (1, 1))):
+        for index, (b, j) in enumerate(((0, 0), (0, 1), (1, 0))):
             light(b, j, index, nc.scalar.copy)
         for block in range(S // BLOCK):
             gated(block)
             if block in (4, 6):
                 quantize(block // 2 - 2)
-        light(0, 2, 4, nc.scalar.copy)
-        light(0, 3, 5, nc.scalar.copy)
+        light(0, 2, 3, nc.scalar.copy)
+        light(0, 3, 4, nc.scalar.copy)
         second_layer(0, (0,), 0)
-        light(1, 3, 6, nc.vector.tensor_copy)
+        light(1, 3, 2, nc.vector.tensor_copy)
         quantize(2)
         scatter_on_vector(0, 0, HALF)
-        light(1, 2, 7, nc.scalar.copy)
+        light(1, 1, 5, nc.scalar.copy)
+        light(1, 2, 6, nc.scalar.copy)
         second_layer(0, (1,), 1)
-        second_layer(1, (0, 1), 4)
-        second_layer(2, (0, 1), 5)
+        second_layer(1, (0, 1), 3)
+        second_layer(2, (0, 1), 4)
         scatter_on_scalar(1, 0, WIDE)
         scatter_on_vector(0, HALF, HALF)
         nc.sync.dma_start(out=out[0:P, :], in_=window[0][:])

@@ -26,8 +26,8 @@ HALF = 512
 WIDE = 384
 PER_COL = 16
 W1, W3 = 0, 1
-LINEAR_BANKS = (3, 4, 0, 1, 3, 4, 0, 1)
-GATE_BANKS = (5, 6, 2, 7, 5, 6, 2, 7)
+LINEAR_BANKS = (4, 5, 0, 1, 4, 5, 0, 1)
+GATE_BANKS = (6, 7, 2, 3, 6, 7, 2, 3)
 
 
 def load_scale_rows(queues, plane, rows):
@@ -60,30 +60,28 @@ def tile_moe_cas_glu_relu_kernel(
         width = 2 * H + N
         staged = keep.tile([16, width], U8, name="staged", align_bytes=64)
         planes = kept("planes", width, U8)
-        raw = [reuse.tile([P, 2 * H], U8, name="raw%d" % m, offset=m * 2 * H, align_bytes=64) for m in (W1, W3)]
+        raw = [reuse.tile([P, 2 * H], U8, name="raw1", offset=0, align_bytes=64), kept("raw3", 2 * H, U8)]
         up = [kept("up%d" % m, 2 * H, U8) for m in (W1, W3)]
 
         def list_part(first, count):
             return offsets[:, first // PER_COL : (first + count) // PER_COL]
 
-        nc.vector.memset(xs[:].bitcast(I32), 0)
+        for plane in (xs, planes):
+            nc.vector.memset(plane[:].bitcast(I32), 0)
         words = x_words[0].rearrange("p t d -> p (t d)").bitcast(I32)
         nc.gpsimd.dma_start(out=xw[:, : T // 2], in_=words[:, : T // 2])
-        for plane in (planes[:, :H], planes[:, H : 2 * H], planes[:, 2 * H :], w2_plane[:]):
-            nc.gpsimd.memset(plane.bitcast(I32), 0)
-        nc.gpsimd.dma_start(out=xw[:, T // 2 :], in_=words[:, T // 2 :])
+        nc.gpsimd.dma_start(out=raw[W3][:].bitcast(I32), in_=w3_words[0].bitcast(I32))
+        nc.gpsimd.memset(w2_plane[:].bitcast(I32), 0)
+        nc.sync.dma_start(out=staged[:, 2 * H :].bitcast(I32), in_=w_scales[0].bitcast(I32))
+        nc.scalar.dma_start(out=staged[:, H : 2 * H].bitcast(I32), in_=w3_scales[0].bitcast(I32))
         nc.sync.dma_start(offsets[:], offs)
-        lo = 0
-        for queue, source in ((nc.scalar, w1_scales), (nc.sync, w3_scales), (nc.scalar, w_scales)):
-            hi = lo + source.shape[2]
-            queue.dma_start(out=staged[:, lo:hi].bitcast(I32), in_=source[0].bitcast(I32))
-            lo = hi
-        load_scale_rows([nc.sync, nc.scalar] * 2, xs, x_scales[0])
-        nc.sync.dma_start(out=raw[W3][:].bitcast(I32), in_=w3_words[0].bitcast(I32))
-        nc.scalar.dma_start(out=raw[W1][:].bitcast(I32), in_=w1_words[0].bitcast(I32))
+        nc.scalar.dma_start(out=staged[:, :H].bitcast(I32), in_=w1_scales[0].bitcast(I32))
+        load_scale_rows([nc.sync, nc.scalar, nc.sync, nc.sync], xs, x_scales[0])
         nc.sync.dma_start(out=ww[:].bitcast(I32), in_=w_words[0].bitcast(I32))
         for r, queue in enumerate([nc.scalar, nc.sync] * 2):
             queue.dma_start(out=planes[r:P:32, :].bitcast(I32), in_=staged[r:16:4, :].bitcast(I32))
+        nc.sync.dma_start(out=xw[:, T // 2 :], in_=words[:, T // 2 :])
+        nc.sync.dma_start(out=raw[W1][:].bitcast(I32), in_=w1_words[0].bitcast(I32))
         nc.sync.dma_start(out=w2w[:].bitcast(I32), in_=w2_words[0].bitcast(I32))
         load_scale_rows([nc.sync] * 4, w2_plane, w2_scales[0])
         w_plane = planes[:, 2 * H :]
@@ -92,18 +90,31 @@ def tile_moe_cas_glu_relu_kernel(
         nc.vector.tensor_copy(gs[:], xs[:].indirect(offsets[:]))
         ups = kept("ups", 2 * H, U8)
         for m in (W3, W1):
-            nc.vector.tensor_copy(
-                out=up[m][:].bitcast(U16).rearrange("p (t m) -> p t m", t=PACK),
-                in_=raw[m][:].bitcast(U16).rearrange("p (m t) -> p t m", t=PACK),
-            )
-        for m in (W3, W1):
             nc.gpsimd.tensor_copy(
                 out=ups[:, m * H : (m + 1) * H].rearrange("p (t m) -> p t m", t=PACK),
                 in_=planes[:, m * H : (m + 1) * H].rearrange("p (m t) -> p t m", t=PACK),
             )
-        gw = reuse.tile([P, S], U32, name="gw", offset=0, align_bytes=64)
-        for first, count in ((0, CHUNK), (CHUNK, CHUNK), (HALF, HALF)):
-            nc.vector.tensor_copy(gw[:, first : first + count], xw[:].bitcast(U32).indirect(list_part(first, count)))
+
+        def permute_words(engine, m):
+            engine.tensor_copy(
+                out=up[m][:].bitcast(U16).rearrange("p (t m) -> p t m", t=PACK),
+                in_=raw[m][:].bitcast(U16).rearrange("p (m t) -> p t m", t=PACK),
+            )
+
+        def gather_words(into, first, count):
+            nc.vector.tensor_copy(into, xw[:].bitcast(U32).indirect(list_part(first, count)))
+
+        permute_words(nc.gpsimd, W3)
+        gw_first = kept("gw_first", CHUNK, U32)
+        gather_words(gw_first[:], 0, CHUNK)
+        permute_words(nc.vector, W1)
+        gw_rest = reuse.tile([P, S - CHUNK], U32, name="gw_rest", offset=0, align_bytes=64)
+        gather_words(gw_rest[:, :CHUNK], CHUNK, CHUNK)
+        gather_words(gw_rest[:, CHUNK:], HALF, HALF)
+
+        def gathered(block):
+            lo = block * BLOCK
+            return gw_first[:, lo : lo + BLOCK] if lo < CHUNK else gw_rest[:, lo - CHUNK : lo - CHUNK + BLOCK]
 
         window = [kept("window0", T, F32), kept("window1", T, F32)]
 
@@ -129,7 +140,7 @@ def tile_moe_cas_glu_relu_kernel(
                     out=acc[:, t, :],
                     lhsT=up[matrix][:, 2 * col : 2 * (col + P)].bitcast(FP4X4),
                     lhsT_scale=ups[:, matrix * H + col : matrix * H + col + P],
-                    rhs=gw[:, block * BLOCK : (block + 1) * BLOCK].bitcast(FP8X4),
+                    rhs=gathered(block).bitcast(FP8X4),
                     rhs_scale=gs[:, block * BLOCK : (block + 1) * BLOCK],
                     start=True,
                     stop=True,
@@ -190,26 +201,25 @@ def tile_moe_cas_glu_relu_kernel(
                 func=ACT.Copy,
             )
 
-        for index, (b, j) in enumerate(((0, 0), (0, 1), (1, 0))):
+        for index, (b, j) in enumerate(((0, 0), (0, 1), (1, 0), (1, 1))):
             light(b, j, index, nc.scalar.copy)
         for block in range(S // BLOCK):
             gated(block)
             if block in (4, 6):
                 quantize(block // 2 - 2)
-        light(0, 2, 3, nc.scalar.copy)
-        light(0, 3, 4, nc.scalar.copy)
+        light(0, 2, 4, nc.scalar.copy)
+        light(0, 3, 5, nc.scalar.copy)
         second_layer(0, (0,), 0)
-        light(1, 3, 2, nc.vector.tensor_copy)
+        light(1, 3, 6, nc.vector.tensor_copy)
         quantize(2)
         scatter_on_vector(0, 0, HALF)
-        light(1, 1, 5, nc.scalar.copy)
-        light(1, 2, 6, nc.scalar.copy)
+        light(1, 2, 7, nc.scalar.copy)
         second_layer(0, (1,), 1)
-        second_layer(1, (0, 1), 3)
-        second_layer(2, (0, 1), 4)
+        second_layer(1, (0, 1), 4)
+        second_layer(2, (0, 1), 5)
         scatter_on_scalar(1, 0, WIDE)
         scatter_on_vector(0, HALF, HALF)
         nc.sync.dma_start(out=out[0:P, :], in_=window[0][:])
         scatter_on_scalar(1, S - WIDE, WIDE)
         scatter_on_scalar(1, WIDE, S - 2 * WIDE)
-        nc.sync.dma_start(out=out[P : 2 * P, :], in_=window[1][:])
+        nc.scalar.dma_start(out=out[P : 2 * P, :], in_=window[1][:])

@@ -24,6 +24,7 @@ BLOCK = 128
 CHUNK = 256
 HALF = 512
 WIDE = 384
+SHARE = 256
 PER_COL = 16
 W1, W3 = 0, 1
 LINEAR_BANKS = (4, 5, 0, 1, 4, 5, 0, 1)
@@ -118,9 +119,9 @@ def tile_moe_cas_glu_relu_kernel(
 
         window = [kept("window0", T, F32), kept("window1", T, F32)]
 
-        def light(b, j, index, evacuate):
-            cols = slice(j * BANK, (j + 1) * BANK)
-            acc = bank("light%d_%d" % (b, j), [P, BANK], index)
+        def light(b, first, count, index, evacuate):
+            cols = slice(first, first + count)
+            acc = bank("light%d_%d" % (b, first), [P, count], index)
             nc.tensor.matmul_mx(
                 out=acc[:],
                 lhsT=ww[:, 2 * P * b : 2 * P * (b + 1)].bitcast(FP4X4),
@@ -202,18 +203,19 @@ def tile_moe_cas_glu_relu_kernel(
             )
 
         for index, (b, j) in enumerate(((0, 0), (0, 1), (1, 0), (1, 1))):
-            light(b, j, index, nc.scalar.copy)
+            light(b, j * BANK, BANK, index, nc.scalar.copy)
         for block in range(S // BLOCK):
             gated(block)
             if block in (4, 6):
                 quantize(block // 2 - 2)
-        light(0, 2, 4, nc.scalar.copy)
-        light(0, 3, 5, nc.scalar.copy)
+        light(0, 2 * BANK, BANK, 4, nc.scalar.copy)
+        light(0, 3 * BANK, BANK, 5, nc.scalar.copy)
         second_layer(0, (0,), 0)
-        light(1, 3, 6, nc.vector.tensor_copy)
+        light(1, T - SHARE, SHARE, 6, nc.vector.tensor_copy)
         quantize(2)
         scatter_on_vector(0, 0, HALF)
-        light(1, 2, 7, nc.scalar.copy)
+        light(1, 2 * BANK, BANK, 7, nc.scalar.copy)
+        light(1, 3 * BANK, BANK - SHARE, 2, nc.scalar.copy)
         second_layer(0, (1,), 1)
         second_layer(1, (0, 1), 4)
         second_layer(2, (0, 1), 5)

@@ -174,21 +174,20 @@ def tile_moe_cas_glu_relu_kernel(
         def quantize(part):
             nc.vector.quantize_mx(out=codes[part][:].bitcast(FP8X4), scales=scales[part][:], in_=hidden[part][:])
 
-        def second_layer(part, row_blocks, index):
-            first, count = parts[part]
-            acc = bank("down%d_%d" % (part, row_blocks[0]), [P, len(row_blocks), count], index)
-            for at, b in enumerate(row_blocks):
-                nc.tensor.matmul_mx(
-                    out=acc[:, at, :],
-                    lhsT=w2w[:, 2 * P * b : 2 * P * (b + 1)].bitcast(FP4X4),
-                    lhsT_scale=w2_plane[:, P * b : P * (b + 1)],
-                    rhs=codes[part][:].bitcast(FP8X4),
-                    rhs_scale=scales[part][:],
-                    start=True,
-                    stop=True,
-                )
-            rows = z[:].rearrange("p (b s) -> p b s", b=2)[:, row_blocks[0] : row_blocks[-1] + 1, first : first + count]
-            nc.scalar.copy(out=rows, in_=acc[:])
+        def second_layer(b, half, index):
+            acc = bank("down%d_%d" % (b, half), [P, HALF], index)
+            for part, (first, count) in enumerate(parts):
+                if first // HALF == half:
+                    nc.tensor.matmul_mx(
+                        out=acc[:, first % HALF : first % HALF + count],
+                        lhsT=w2w[:, 2 * P * b : 2 * P * (b + 1)].bitcast(FP4X4),
+                        lhsT_scale=w2_plane[:, P * b : P * (b + 1)],
+                        rhs=codes[part][:].bitcast(FP8X4),
+                        rhs_scale=scales[part][:],
+                        start=True,
+                        stop=True,
+                    )
+            nc.scalar.copy(out=z[:, b * S + half * HALF : b * S + (half + 1) * HALF], in_=acc[:])
 
         def scatter_on_vector(b, first, count):
             nc.vector.tensor_copy(
@@ -210,18 +209,18 @@ def tile_moe_cas_glu_relu_kernel(
                 quantize(block // 2 - 2)
         light(0, 2 * BANK, BANK, 4, nc.scalar.copy)
         light(0, 3 * BANK, BANK, 5, nc.scalar.copy)
-        second_layer(0, (0,), 0)
+        second_layer(0, 0, 0)
         light(1, T - SHARE, SHARE, 6, nc.vector.tensor_copy)
         quantize(2)
         scatter_on_vector(0, 0, HALF)
         light(1, 2 * BANK, BANK, 7, nc.scalar.copy)
         light(1, 3 * BANK, BANK - SHARE, 2, nc.scalar.copy)
-        second_layer(0, (1,), 1)
-        second_layer(1, (0, 1), 4)
-        second_layer(2, (0, 1), 5)
-        scatter_on_scalar(1, 0, WIDE)
+        second_layer(1, 0, 1)
+        second_layer(1, 1, 4)
+        scatter_on_scalar(1, 0, CHUNK)
+        second_layer(0, 1, 5)
         scatter_on_vector(0, HALF, HALF)
         nc.sync.dma_start(out=out[0:P, :], in_=window[0][:])
-        scatter_on_scalar(1, S - WIDE, WIDE)
-        scatter_on_scalar(1, WIDE, S - 2 * WIDE)
+        scatter_on_scalar(1, CHUNK, WIDE)
+        scatter_on_scalar(1, CHUNK + WIDE, WIDE)
         nc.scalar.dma_start(out=out[P : 2 * P, :], in_=window[1][:])

@@ -59,10 +59,10 @@ def tile_moe_cas_glu_relu_kernel(
         w2w = kept("w2w", 2 * N, U8)
         w2_plane = kept("w2_plane", N, U8)
         width = 2 * H + N
-        staged = keep.tile([16, width], U8, name="staged", align_bytes=64)
+        staged = reuse.tile([16, width], U8, name="staged", offset=0, align_bytes=64)
         planes = kept("planes", width, U8)
-        raw = [reuse.tile([P, 2 * H], U8, name="raw1", offset=0, align_bytes=64), kept("raw3", 2 * H, U8)]
-        up = [kept("up%d" % m, 2 * H, U8) for m in (W1, W3)]
+        raw = [kept("raw%d" % m, 2 * H, U8) for m in (W1, W3)]
+        up = [kept("up1", 2 * H, U8), reuse.tile([P, 2 * H], U8, name="up3", offset=0, align_bytes=64)]
 
         def list_part(first, count):
             return offsets[:, first // PER_COL : (first + count) // PER_COL]
@@ -105,11 +105,11 @@ def tile_moe_cas_glu_relu_kernel(
         def gather_words(into, first, count):
             nc.vector.tensor_copy(into, xw[:].bitcast(U32).indirect(list_part(first, count)))
 
-        permute_words(nc.gpsimd, W3)
+        permute_words(nc.vector, W3)
         gw_first = kept("gw_first", CHUNK, U32)
         gather_words(gw_first[:], 0, CHUNK)
-        permute_words(nc.vector, W1)
-        gw_rest = reuse.tile([P, S - CHUNK], U32, name="gw_rest", offset=0, align_bytes=64)
+        permute_words(nc.gpsimd, W1)
+        gw_rest = kept("gw_rest", S - CHUNK, U32)
         gather_words(gw_rest[:, :CHUNK], CHUNK, CHUNK)
         gather_words(gw_rest[:, CHUNK:], HALF, HALF)
 

@@ -43,7 +43,6 @@ def tile_moe_cas_glu_relu_kernel(
     nc = tc.nc
     with ExitStack() as ctx:
         keep = ctx.enter_context(tc.tile_pool(name="keep", bufs=1))
-        reuse = ctx.enter_context(tc.tile_pool(name="reuse", bufs=1))
         psum = ctx.enter_context(tc.psum_pool(name="psum", bufs=1))
 
         def kept(name, width, dtype):
@@ -58,46 +57,53 @@ def tile_moe_cas_glu_relu_kernel(
         ww = kept("ww", 2 * N, U8)
         w2w = kept("w2w", 2 * N, U8)
         w2_plane = kept("w2_plane", N, U8)
-        width = 2 * H + N
-        staged = reuse.tile([16, width], U8, name="staged", offset=0, align_bytes=64)
-        planes = kept("planes", width, U8)
+        w_rows = keep.tile([4, 4 * N], U8, name="w_rows", align_bytes=64)
+        w_plane = kept("w_plane", N, U8)
+        staged = kept("staged", 2 * H, U8)
+        ordered = kept("ordered", 2 * H, U8)
+        ups = kept("ups", 2 * H, U8)
         raw = [kept("raw%d" % m, 2 * H, U8) for m in (W1, W3)]
-        up = [kept("up1", 2 * H, U8), reuse.tile([P, 2 * H], U8, name="up3", offset=0, align_bytes=64)]
+        up = [kept("up%d" % m, 2 * H, U8) for m in (W1, W3)]
 
         def list_part(first, count):
             return offsets[:, first // PER_COL : (first + count) // PER_COL]
 
-        for plane in (xs, planes):
+        for plane in (staged, xs, w_plane, ups):
             nc.vector.memset(plane[:].bitcast(I32), 0)
         words = x_words[0].rearrange("p t d -> p (t d)").bitcast(I32)
         nc.gpsimd.dma_start(out=xw[:, : T // 2], in_=words[:, : T // 2])
-        nc.gpsimd.dma_start(out=raw[W3][:].bitcast(I32), in_=w3_words[0].bitcast(I32))
         nc.gpsimd.memset(w2_plane[:].bitcast(I32), 0)
-        nc.sync.dma_start(out=staged[:, 2 * H :].bitcast(I32), in_=w_scales[0].bitcast(I32))
-        nc.scalar.dma_start(out=staged[:, H : 2 * H].bitcast(I32), in_=w3_scales[0].bitcast(I32))
+        nc.sync.dma_start(
+            out=w_rows[:].bitcast(I32).rearrange("r (q c) -> r q c", q=4),
+            in_=w_scales[0].rearrange("(q r) c -> r q c", r=4).bitcast(I32),
+        )
+        nc.scalar.dma_start(out=staged[:16, H:].bitcast(I32), in_=w3_scales[0].bitcast(I32))
         nc.sync.dma_start(offsets[:], offs)
-        nc.scalar.dma_start(out=staged[:, :H].bitcast(I32), in_=w1_scales[0].bitcast(I32))
-        load_scale_rows([nc.sync, nc.scalar, nc.sync, nc.sync], xs, x_scales[0])
+        nc.scalar.dma_start(out=staged[:16, :H].bitcast(I32), in_=w1_scales[0].bitcast(I32))
+        load_scale_rows([nc.sync, nc.scalar] * 2, xs, x_scales[0])
         nc.sync.dma_start(out=ww[:].bitcast(I32), in_=w_words[0].bitcast(I32))
-        for r, queue in enumerate([nc.scalar, nc.sync] * 2):
-            queue.dma_start(out=planes[r:P:32, :].bitcast(I32), in_=staged[r:16:4, :].bitcast(I32))
+        nc.sync.dma_start(out=raw[W3][:].bitcast(I32), in_=w3_words[0].bitcast(I32))
         nc.sync.dma_start(out=xw[:, T // 2 :], in_=words[:, T // 2 :])
-        nc.sync.dma_start(out=raw[W1][:].bitcast(I32), in_=w1_words[0].bitcast(I32))
         nc.sync.dma_start(out=w2w[:].bitcast(I32), in_=w2_words[0].bitcast(I32))
+
+        for q in range(4):
+            nc.vector.tensor_copy(
+                out=w_plane[32 * q : 32 * q + 4, :].bitcast(I32), in_=w_rows[:, q * N : (q + 1) * N].bitcast(I32)
+            )
+        nc.vector.tensor_copy(
+            out=ordered[:].rearrange("p (w t m) -> p w t m", w=2, t=PACK),
+            in_=staged[:].rearrange("p (w m t) -> p w t m", w=2, t=PACK),
+        )
+        for r in range(4):
+            nc.sync.dma_start(out=ups[r:P:32, :].bitcast(I32), in_=ordered[r:16:4, :].bitcast(I32))
+        nc.sync.dma_start(out=raw[W1][:].bitcast(I32), in_=w1_words[0].bitcast(I32))
         load_scale_rows([nc.sync] * 4, w2_plane, w2_scales[0])
-        w_plane = planes[:, 2 * H :]
 
         gs = kept("gs", S, U8)
         nc.vector.tensor_copy(gs[:], xs[:].indirect(offsets[:]))
-        ups = kept("ups", 2 * H, U8)
-        for m in (W3, W1):
-            nc.gpsimd.tensor_copy(
-                out=ups[:, m * H : (m + 1) * H].rearrange("p (t m) -> p t m", t=PACK),
-                in_=planes[:, m * H : (m + 1) * H].rearrange("p (m t) -> p t m", t=PACK),
-            )
 
-        def permute_words(engine, m):
-            engine.tensor_copy(
+        def permute_words(copy, m):
+            copy(
                 out=up[m][:].bitcast(U16).rearrange("p (t m) -> p t m", t=PACK),
                 in_=raw[m][:].bitcast(U16).rearrange("p (m t) -> p t m", t=PACK),
             )
@@ -105,12 +111,12 @@ def tile_moe_cas_glu_relu_kernel(
         def gather_words(into, first, count):
             nc.vector.tensor_copy(into, xw[:].bitcast(U32).indirect(list_part(first, count)))
 
-        permute_words(nc.vector, W3)
+        permute_words(nc.scalar.copy, W3)
         gw_first = kept("gw_first", CHUNK, U32)
         gather_words(gw_first[:], 0, CHUNK)
-        permute_words(nc.gpsimd, W1)
         gw_rest = kept("gw_rest", S - CHUNK, U32)
         gather_words(gw_rest[:, :CHUNK], CHUNK, CHUNK)
+        permute_words(nc.vector.tensor_copy, W1)
         gather_words(gw_rest[:, CHUNK:], HALF, HALF)
 
         def gathered(block):

@@ -43,6 +43,8 @@ def tile_moe_cas_glu_relu_kernel(
     nc = tc.nc
     with ExitStack() as ctx:
         keep = ctx.enter_context(tc.tile_pool(name="keep", bufs=1))
+        reuse = ctx.enter_context(tc.tile_pool(name="reuse", bufs=1))
+        late = ctx.enter_context(tc.tile_pool(name="late", bufs=1))
         psum = ctx.enter_context(tc.psum_pool(name="psum", bufs=1))
 
         def kept(name, width, dtype):
@@ -55,15 +57,15 @@ def tile_moe_cas_glu_relu_kernel(
         xw = kept("xw", T, I32)
         xs = kept("xs", T, U8)
         ww = kept("ww", 2 * N, U8)
-        w2w = kept("w2w", 2 * N, U8)
-        w2_plane = kept("w2_plane", N, U8)
+        w2w = reuse.tile([P, 2 * N], U8, name="w2w", offset=2 * H, align_bytes=64)
+        w2_plane = reuse.tile([P, N], U8, name="w2_plane", offset=2 * H + 2 * N, align_bytes=64)
         w_rows = keep.tile([4, 4 * N], U8, name="w_rows", align_bytes=64)
         w_plane = kept("w_plane", N, U8)
-        staged = kept("staged", 2 * H, U8)
-        ordered = kept("ordered", 2 * H, U8)
+        staged = reuse.tile([P, 2 * H], U8, name="staged", offset=2 * H - 64, align_bytes=64)
+        ordered = late.tile([P, 2 * H], U8, name="ordered", offset=4 * HALF, align_bytes=64)
         ups = kept("ups", 2 * H, U8)
-        raw = [kept("raw%d" % m, 2 * H, U8) for m in (W1, W3)]
-        up = [kept("up%d" % m, 2 * H, U8) for m in (W1, W3)]
+        raw = [late.tile([P, 2 * H], U8, name="raw1", offset=0, align_bytes=64), kept("raw3", 2 * H, U8)]
+        up = [late.tile([P, 2 * H], U8, name="up1", offset=4 * HALF, align_bytes=64), kept("up3", 2 * H, U8)]
 
         def list_part(first, count):
             return offsets[:, first // PER_COL : (first + count) // PER_COL]
@@ -72,7 +74,7 @@ def tile_moe_cas_glu_relu_kernel(
             nc.vector.memset(plane[:].bitcast(I32), 0)
         words = x_words[0].rearrange("p t d -> p (t d)").bitcast(I32)
         nc.gpsimd.dma_start(out=xw[:, : T // 2], in_=words[:, : T // 2])
-        nc.gpsimd.memset(w2_plane[:].bitcast(I32), 0)
+        nc.gpsimd.dma_start(out=raw[W1][:].bitcast(I32), in_=w1_words[0].bitcast(I32))
         nc.sync.dma_start(
             out=w_rows[:].bitcast(I32).rearrange("r (q c) -> r q c", q=4),
             in_=w_scales[0].rearrange("(q r) c -> r q c", r=4).bitcast(I32),
@@ -82,11 +84,11 @@ def tile_moe_cas_glu_relu_kernel(
         nc.scalar.dma_start(out=staged[:16, :H].bitcast(I32), in_=w1_scales[0].bitcast(I32))
         load_scale_rows([nc.sync, nc.scalar] * 2, xs, x_scales[0])
         nc.sync.dma_start(out=ww[:].bitcast(I32), in_=w_words[0].bitcast(I32))
-        nc.sync.dma_start(out=raw[W3][:].bitcast(I32), in_=w3_words[0].bitcast(I32))
         nc.sync.dma_start(out=xw[:, T // 2 :], in_=words[:, T // 2 :])
-        nc.sync.dma_start(out=w2w[:].bitcast(I32), in_=w2_words[0].bitcast(I32))
+        nc.sync.dma_start(out=raw[W3][:].bitcast(I32), in_=w3_words[0].bitcast(I32))
 
-        for q in range(4):
+        nc.scalar.copy(out=w_plane[:4, :].bitcast(U32), in_=w_rows[:, :N].bitcast(U32))
+        for q in range(1, 4):
             nc.vector.tensor_copy(
                 out=w_plane[32 * q : 32 * q + 4, :].bitcast(I32), in_=w_rows[:, q * N : (q + 1) * N].bitcast(I32)
             )
@@ -94,9 +96,10 @@ def tile_moe_cas_glu_relu_kernel(
             out=ordered[:].rearrange("p (w t m) -> p w t m", w=2, t=PACK),
             in_=staged[:].rearrange("p (w m t) -> p w t m", w=2, t=PACK),
         )
-        for r in range(4):
-            nc.sync.dma_start(out=ups[r:P:32, :].bitcast(I32), in_=ordered[r:16:4, :].bitcast(I32))
-        nc.sync.dma_start(out=raw[W1][:].bitcast(I32), in_=w1_words[0].bitcast(I32))
+        for r, queue in enumerate([nc.scalar, nc.sync] * 2):
+            queue.dma_start(out=ups[r:P:32, :].bitcast(I32), in_=ordered[r:16:4, :].bitcast(I32))
+        nc.sync.dma_start(out=w2w[:].bitcast(I32), in_=w2_words[0].bitcast(I32))
+        nc.gpsimd.memset(w2_plane[:].bitcast(I32), 0)
         load_scale_rows([nc.sync] * 4, w2_plane, w2_scales[0])
 
         gs = kept("gs", S, U8)
@@ -111,17 +114,17 @@ def tile_moe_cas_glu_relu_kernel(
         def gather_words(into, first, count):
             nc.vector.tensor_copy(into, xw[:].bitcast(U32).indirect(list_part(first, count)))
 
-        permute_words(nc.scalar.copy, W3)
-        gw_first = kept("gw_first", CHUNK, U32)
-        gather_words(gw_first[:], 0, CHUNK)
-        gw_rest = kept("gw_rest", S - CHUNK, U32)
-        gather_words(gw_rest[:, :CHUNK], CHUNK, CHUNK)
+        gw_first = kept("gw_first", HALF, U32)
+        gather_words(gw_first[:, :CHUNK], 0, CHUNK)
+        permute_words(nc.vector.tensor_copy, W3)
+        gather_words(gw_first[:, CHUNK:], CHUNK, CHUNK)
         permute_words(nc.vector.tensor_copy, W1)
-        gather_words(gw_rest[:, CHUNK:], HALF, HALF)
+        gw_rest = late.tile([P, HALF], U32, name="gw_rest", offset=0, align_bytes=64)
+        gather_words(gw_rest[:], HALF, HALF)
 
         def gathered(block):
             lo = block * BLOCK
-            return gw_first[:, lo : lo + BLOCK] if lo < CHUNK else gw_rest[:, lo - CHUNK : lo - CHUNK + BLOCK]
+            return gw_first[:, lo : lo + BLOCK] if lo < HALF else gw_rest[:, lo - HALF : lo - HALF + BLOCK]
 
         window = [kept("window0", T, F32), kept("window1", T, F32)]
 

@@ -57,15 +57,18 @@ def tile_moe_cas_glu_relu_kernel(
         xw = kept("xw", T, I32)
         xs = kept("xs", T, U8)
         ww = kept("ww", 2 * N, U8)
-        w2w = reuse.tile([P, 2 * N], U8, name="w2w", offset=2 * H, align_bytes=64)
-        w2_plane = reuse.tile([P, N], U8, name="w2_plane", offset=2 * H + 2 * N, align_bytes=64)
+        w2w = reuse.tile([P, 2 * N], U8, name="w2w", offset=4 * H, align_bytes=64)
+        w2_plane = reuse.tile([P, N], U8, name="w2_plane", offset=4 * H + 2 * N, align_bytes=64)
         w_rows = keep.tile([4, 4 * N], U8, name="w_rows", align_bytes=64)
         w_plane = kept("w_plane", N, U8)
-        staged = reuse.tile([P, 2 * H], U8, name="staged", offset=2 * H - 64, align_bytes=64)
-        ordered = late.tile([P, 2 * H], U8, name="ordered", offset=4 * HALF, align_bytes=64)
+        staged = reuse.tile([P, 2 * H], U8, name="staged", offset=4 * H - 64, align_bytes=64)
+        ordered = late.tile([P, 2 * H], U8, name="ordered", offset=2 * H, align_bytes=64)
         ups = kept("ups", 2 * H, U8)
-        raw = [late.tile([P, 2 * H], U8, name="raw1", offset=0, align_bytes=64), kept("raw3", 2 * H, U8)]
-        up = [late.tile([P, 2 * H], U8, name="up1", offset=4 * HALF, align_bytes=64), kept("up3", 2 * H, U8)]
+        raw = [
+            reuse.tile([P, 2 * H], U8, name="raw1", offset=2 * H, align_bytes=64),
+            late.tile([P, 2 * H], U8, name="raw3", offset=0, align_bytes=64),
+        ]
+        up = [kept("up1", 2 * H, U8), late.tile([P, 2 * H], U8, name="up3", offset=2 * H, align_bytes=64)]
 
         def list_part(first, count):
             return offsets[:, first // PER_COL : (first + count) // PER_COL]
@@ -74,7 +77,7 @@ def tile_moe_cas_glu_relu_kernel(
             nc.vector.memset(plane[:].bitcast(I32), 0)
         words = x_words[0].rearrange("p t d -> p (t d)").bitcast(I32)
         nc.gpsimd.dma_start(out=xw[:, : T // 2], in_=words[:, : T // 2])
-        nc.gpsimd.dma_start(out=raw[W1][:].bitcast(I32), in_=w1_words[0].bitcast(I32))
+        nc.gpsimd.dma_start(out=raw[W3][:].bitcast(I32), in_=w3_words[0].bitcast(I32))
         nc.sync.dma_start(
             out=w_rows[:].bitcast(I32).rearrange("r (q c) -> r q c", q=4),
             in_=w_scales[0].rearrange("(q r) c -> r q c", r=4).bitcast(I32),
@@ -85,7 +88,6 @@ def tile_moe_cas_glu_relu_kernel(
         load_scale_rows([nc.sync, nc.scalar] * 2, xs, x_scales[0])
         nc.sync.dma_start(out=ww[:].bitcast(I32), in_=w_words[0].bitcast(I32))
         nc.sync.dma_start(out=xw[:, T // 2 :], in_=words[:, T // 2 :])
-        nc.sync.dma_start(out=raw[W3][:].bitcast(I32), in_=w3_words[0].bitcast(I32))
 
         nc.scalar.copy(out=w_plane[:4, :].bitcast(U32), in_=w_rows[:, :N].bitcast(U32))
         for q in range(1, 4):
@@ -98,6 +100,7 @@ def tile_moe_cas_glu_relu_kernel(
         )
         for r, queue in enumerate([nc.scalar, nc.sync] * 2):
             queue.dma_start(out=ups[r:P:32, :].bitcast(I32), in_=ordered[r:16:4, :].bitcast(I32))
+        nc.sync.dma_start(out=raw[W1][:].bitcast(I32), in_=w1_words[0].bitcast(I32))
         nc.sync.dma_start(out=w2w[:].bitcast(I32), in_=w2_words[0].bitcast(I32))
         nc.gpsimd.memset(w2_plane[:].bitcast(I32), 0)
         load_scale_rows([nc.sync] * 4, w2_plane, w2_scales[0])
@@ -114,17 +117,21 @@ def tile_moe_cas_glu_relu_kernel(
         def gather_words(into, first, count):
             nc.vector.tensor_copy(into, xw[:].bitcast(U32).indirect(list_part(first, count)))
 
-        gw_first = kept("gw_first", HALF, U32)
-        gather_words(gw_first[:, :CHUNK], 0, CHUNK)
+        gw = [
+            kept("gw0", CHUNK, U32),
+            late.tile([P, CHUNK], U32, name="gw1", offset=0, align_bytes=64),
+            reuse.tile([P, HALF], U32, name="gw2", offset=0, align_bytes=64),
+        ]
+        gather_words(gw[0][:], 0, CHUNK)
         permute_words(nc.vector.tensor_copy, W3)
-        gather_words(gw_first[:, CHUNK:], CHUNK, CHUNK)
+        gather_words(gw[1][:], CHUNK, CHUNK)
         permute_words(nc.vector.tensor_copy, W1)
-        gw_rest = late.tile([P, HALF], U32, name="gw_rest", offset=0, align_bytes=64)
-        gather_words(gw_rest[:], HALF, HALF)
+        gather_words(gw[2][:], HALF, HALF)
 
         def gathered(block):
-            lo = block * BLOCK
-            return gw_first[:, lo : lo + BLOCK] if lo < HALF else gw_rest[:, lo - HALF : lo - HALF + BLOCK]
+            piece = min(block * BLOCK // CHUNK, 2)
+            lo = block * BLOCK - piece * CHUNK
+            return gw[piece][:, lo : lo + BLOCK]
 
         window = [kept("window0", T, F32), kept("window1", T, F32)]
 
@@ -210,7 +217,9 @@ def tile_moe_cas_glu_relu_kernel(
                 func=ACT.Copy,
             )
 
-        for index, (b, j) in enumerate(((0, 0), (0, 1), (1, 0), (1, 1))):
+        light(0, 0, CHUNK, 7, nc.scalar.copy)
+        light(0, CHUNK, CHUNK, 0, nc.scalar.copy)
+        for index, (b, j) in enumerate(((0, 1), (1, 0), (1, 1)), start=1):
             light(b, j * BANK, BANK, index, nc.scalar.copy)
         for block in range(S // BLOCK):
             gated(block)

@@ -102,7 +102,6 @@ def tile_moe_cas_glu_relu_kernel(
             queue.dma_start(out=ups[r:P:32, :].bitcast(I32), in_=ordered[r:16:4, :].bitcast(I32))
         nc.sync.dma_start(out=raw[W1][:].bitcast(I32), in_=w1_words[0].bitcast(I32))
         nc.sync.dma_start(out=w2w[:].bitcast(I32), in_=w2_words[0].bitcast(I32))
-        nc.gpsimd.memset(w2_plane[:].bitcast(I32), 0)
         load_scale_rows([nc.sync] * 4, w2_plane, w2_scales[0])
 
         gs = kept("gs", S, U8)

from contextlib import ExitStack

import concourse.mybir as mybir

K, T, S, H, N = 512, 2048, 1024, 512, 256
FLOPS = 2 * K * N * T + 2 * 2 * K * H * S + 2 * H * N * S

F32 = mybir.dt.float32
BF16 = mybir.dt.bfloat16
I32 = mybir.dt.int32
U32 = mybir.dt.uint32
U16 = mybir.dt.uint16
U8 = mybir.dt.uint8
FP8X4 = mybir.dt.float8_e4m3fn_x4
FP4X4 = mybir.dt.float4_e2m1fn_x4
ALU = mybir.AluOpType
ACT = mybir.ActivationFunctionType

P = 128
PACK = 4
BANK = 512
BANK_BYTES = 2048
BLOCK = 128
CHUNK = 256
HALF = 512
WIDE = 384
SHARE = 256
PER_COL = 16
W1, W3 = 0, 1
LINEAR_BANKS = (4, 5, 0, 1, 4, 5, 0, 1)
GATE_BANKS = (6, 7, 2, 3, 6, 7, 2, 3)


def load_scale_rows(queues, plane, rows):
    by_quadrant = rows.rearrange("(q r) c -> r q c", r=4)
    for r in range(4):
        queues[r].dma_start(out=plane[r:P:32, :].bitcast(I32), in_=by_quadrant[r].bitcast(I32))


def tile_moe_cas_glu_relu_kernel(
    tc, x_words, x_scales, w_words, w_scales, w1_words, w1_scales, w3_words, w3_scales, w2_words, w2_scales, offs, out
):
    nc = tc.nc
    with ExitStack() as ctx:
        keep = ctx.enter_context(tc.tile_pool(name="keep", bufs=1))
        reuse = ctx.enter_context(tc.tile_pool(name="reuse", bufs=1))
        late = ctx.enter_context(tc.tile_pool(name="late", bufs=1))
        psum = ctx.enter_context(tc.psum_pool(name="psum", bufs=1))

        def kept(name, width, dtype):
            return keep.tile([P, width], dtype, name=name, align_bytes=64)

        def bank(name, shape, index):
            return psum.tile(shape, F32, name=name, offset=index * BANK_BYTES)

        offsets = keep.tile([P, S // PER_COL], U16, name="offsets")
        xw = kept("xw", T, I32)
        xs = kept("xs", T, U8)
        ww = kept("ww", 2 * N, U8)
        w2w = reuse.tile([P, 2 * N], U8, name="w2w", offset=4 * H, align_bytes=64)
        w2_plane = reuse.tile([P, N], U8, name="w2_plane", offset=4 * H + 2 * N, align_bytes=64)
        w_rows = keep.tile([4, 4 * N], U8, name="w_rows", align_bytes=64)
        w_plane = kept("w_plane", N, U8)
        staged = reuse.tile([P, 2 * H], U8, name="staged", offset=4 * H - 64, align_bytes=64)
        ordered = late.tile([P, 2 * H], U8, name="ordered", offset=2 * H, align_bytes=64)
        ups = kept("ups", 2 * H, U8)
        raw = [
            reuse.tile([P, 2 * H], U8, name="raw1", offset=2 * H, align_bytes=64),
            late.tile([P, 2 * H], U8, name="raw3", offset=0, align_bytes=64),
        ]
        up = [kept("up1", 2 * H, U8), late.tile([P, 2 * H], U8, name="up3", offset=2 * H, align_bytes=64)]

        def list_part(first, count):
            return offsets[:, first // PER_COL : (first + count) // PER_COL]

        for plane in (staged, xs, w_plane, ups):
            nc.vector.memset(plane[:].bitcast(I32), 0)
        words = x_words[0].rearrange("p t d -> p (t d)").bitcast(I32)
        nc.gpsimd.dma_start(out=xw[:, : T // 2], in_=words[:, : T // 2])
        nc.gpsimd.dma_start(out=raw[W3][:].bitcast(I32), in_=w3_words[0].bitcast(I32))
        nc.sync.dma_start(
            out=w_rows[:].bitcast(I32).rearrange("r (q c) -> r q c", q=4),
            in_=w_scales[0].rearrange("(q r) c -> r q c", r=4).bitcast(I32),
        )
        nc.scalar.dma_start(out=staged[:16, H:].bitcast(I32), in_=w3_scales[0].bitcast(I32))
        nc.sync.dma_start(offsets[:], offs)
        nc.scalar.dma_start(out=staged[:16, :H].bitcast(I32), in_=w1_scales[0].bitcast(I32))
        load_scale_rows([nc.sync, nc.scalar] * 2, xs, x_scales[0])
        nc.sync.dma_start(out=ww[:].bitcast(I32), in_=w_words[0].bitcast(I32))
        nc.sync.dma_start(out=xw[:, T // 2 :], in_=words[:, T // 2 :])

        nc.scalar.copy(out=w_plane[:4, :].bitcast(U32), in_=w_rows[:, :N].bitcast(U32))
        for q in range(1, 4):
            nc.vector.tensor_copy(
                out=w_plane[32 * q : 32 * q + 4, :].bitcast(I32), in_=w_rows[:, q * N : (q + 1) * N].bitcast(I32)
            )
        nc.vector.tensor_copy(
            out=ordered[:].rearrange("p (w t m) -> p w t m", w=2, t=PACK),
            in_=staged[:].rearrange("p (w m t) -> p w t m", w=2, t=PACK),
        )
        for r, queue in enumerate([nc.scalar, nc.sync] * 2):
            queue.dma_start(out=ups[r:P:32, :].bitcast(I32), in_=ordered[r:16:4, :].bitcast(I32))
        nc.sync.dma_start(out=raw[W1][:].bitcast(I32), in_=w1_words[0].bitcast(I32))
        nc.sync.dma_start(out=w2w[:].bitcast(I32), in_=w2_words[0].bitcast(I32))
        load_scale_rows([nc.sync] * 4, w2_plane, w2_scales[0])

        gs = kept("gs", S, U8)
        nc.vector.tensor_copy(gs[:], xs[:].indirect(offsets[:]))

        def permute_words(copy, m):
            copy(
                out=up[m][:].bitcast(U16).rearrange("p (t m) -> p t m", t=PACK),
                in_=raw[m][:].bitcast(U16).rearrange("p (m t) -> p t m", t=PACK),
            )

        def gather_words(into, first, count):
            nc.vector.tensor_copy(into, xw[:].bitcast(U32).indirect(list_part(first, count)))

        gw = [
            kept("gw0", CHUNK, U32),
            late.tile([P, CHUNK], U32, name="gw1", offset=0, align_bytes=64),
            reuse.tile([P, HALF], U32, name="gw2", offset=0, align_bytes=64),
        ]
        gather_words(gw[0][:], 0, CHUNK)
        permute_words(nc.vector.tensor_copy, W3)
        gather_words(gw[1][:], CHUNK, CHUNK)
        permute_words(nc.vector.tensor_copy, W1)
        gather_words(gw[2][:], HALF, HALF)

        def gathered(block):
            piece = min(block * BLOCK // CHUNK, 2)
            lo = block * BLOCK - piece * CHUNK
            return gw[piece][:, lo : lo + BLOCK]

        window = [kept("window0", T, F32), kept("window1", T, F32)]

        def light(b, first, count, index, evacuate):
            cols = slice(first, first + count)
            acc = bank("light%d_%d" % (b, first), [P, count], index)
            nc.tensor.matmul_mx(
                out=acc[:],
                lhsT=ww[:, 2 * P * b : 2 * P * (b + 1)].bitcast(FP4X4),
                lhsT_scale=w_plane[:, P * b : P * (b + 1)],
                rhs=xw[:, cols].bitcast(FP8X4),
                rhs_scale=xs[:, cols],
                start=True,
                stop=True,
            )
            evacuate(out=window[b][:, cols], in_=acc[:])

        def first_layer(matrix, block, index):
            acc = bank("pre%d_%d" % (matrix, block), [P, PACK, BLOCK], index)
            for t in range(PACK):
                col = t * P
                nc.tensor.matmul_mx(
                    out=acc[:, t, :],
                    lhsT=up[matrix][:, 2 * col : 2 * (col + P)].bitcast(FP4X4),
                    lhsT_scale=ups[:, matrix * H + col : matrix * H + col + P],
                    rhs=gathered(block).bitcast(FP8X4),
                    rhs_scale=gs[:, block * BLOCK : (block + 1) * BLOCK],
                    start=True,
                    stop=True,
                )
            return acc[:].rearrange("p t n -> p n t")

        parts = ((0, HALF), (HALF, CHUNK), (HALF + CHUNK, CHUNK))
        hidden = [kept("hidden%d" % i, count * PACK, BF16) for i, (first, count) in enumerate(parts)]
        codes = [kept("codes%d" % i, count, U32) for i, (first, count) in enumerate(parts)]
        scales = [kept("scales%d" % i, count, U8) for i, (first, count) in enumerate(parts)]
        lin = [kept("lin%d" % block, BANK, F32) for block in range(S // BLOCK)]
        z = kept("z", 2 * S, F32)

        def by_token(ap):
            return ap.rearrange("p (n t) -> p n t", t=PACK)

        def gated(block):
            part = max(i for i, (first, count) in enumerate(parts) if first <= block * BLOCK)
            lo = block * BLOCK - parts[part][0]
            nc.scalar.copy(out=by_token(lin[block][:]), in_=first_layer(W3, block, LINEAR_BANKS[block]))
            nc.vector.scalar_tensor_tensor(
                out=by_token(hidden[part][:, lo * PACK : (lo + BLOCK) * PACK]),
                in0=first_layer(W1, block, GATE_BANKS[block]),
                scalar=0.0,
                in1=by_token(lin[block][:]),
                op0=ALU.max,
                op1=ALU.mult,
            )

        def quantize(part):
            nc.vector.quantize_mx(out=codes[part][:].bitcast(FP8X4), scales=scales[part][:], in_=hidden[part][:])

        def second_layer(b, half, index):
            acc = bank("down%d_%d" % (b, half), [P, HALF], index)
            for part, (first, count) in enumerate(parts):
                if first // HALF == half:
                    nc.tensor.matmul_mx(
                        out=acc[:, first % HALF : first % HALF + count],
                        lhsT=w2w[:, 2 * P * b : 2 * P * (b + 1)].bitcast(FP4X4),
                        lhsT_scale=w2_plane[:, P * b : P * (b + 1)],
                        rhs=codes[part][:].bitcast(FP8X4),
                        rhs_scale=scales[part][:],
                        start=True,
                        stop=True,
                    )
            nc.scalar.copy(out=z[:, b * S + half * HALF : b * S + (half + 1) * HALF], in_=acc[:])

        def scatter_on_vector(b, first, count):
            nc.vector.tensor_copy(
                window[b][:].indirect(list_part(first, count)), z[:, b * S + first : b * S + first + count]
            )

        def scatter_on_scalar(b, first, count):
            nc.scalar.activation(
                out=window[b][:].indirect(list_part(first, count)),
                in_=z[:, b * S + first : b * S + first + count],
                func=ACT.Copy,
            )

        light(0, 0, CHUNK, 7, nc.scalar.copy)
        light(0, CHUNK, CHUNK, 0, nc.scalar.copy)
        for index, (b, j) in enumerate(((0, 1), (1, 0), (1, 1)), start=1):
            light(b, j * BANK, BANK, index, nc.scalar.copy)
        for block in range(S // BLOCK):
            gated(block)
            if block in (4, 6):
                quantize(block // 2 - 2)
        light(0, 2 * BANK, BANK, 4, nc.scalar.copy)
        light(0, 3 * BANK, BANK, 5, nc.scalar.copy)
        second_layer(0, 0, 0)
        light(1, T - SHARE, SHARE, 6, nc.vector.tensor_copy)
        quantize(2)
        scatter_on_vector(0, 0, HALF)
        light(1, 2 * BANK, BANK, 7, nc.scalar.copy)
        light(1, 3 * BANK, BANK - SHARE, 2, nc.scalar.copy)
        second_layer(1, 0, 1)
        second_layer(1, 1, 4)
        scatter_on_scalar(1, 0, CHUNK)
        second_layer(0, 1, 5)
        scatter_on_vector(0, HALF, HALF)
        nc.sync.dma_start(out=out[0:P, :], in_=window[0][:])
        scatter_on_scalar(1, CHUNK, WIDE)
        scatter_on_scalar(1, CHUNK + WIDE, WIDE)
        nc.scalar.dma_start(out=out[P : 2 * P, :], in_=window[1][:])
